import numpy as np
import ml_dtypes


def mxq(x, axis, fmt="e4m3"):
    dtype, down = {"e4m3": (ml_dtypes.float8_e4m3fn, 7), "e5m2": (ml_dtypes.float8_e5m2, 14)}[fmt]
    v = np.moveaxis(np.asarray(x, np.float32).astype(ml_dtypes.bfloat16).astype(np.float64), axis, -1)
    blocks = v.reshape(v.shape[:-1] + (-1, 32))
    amax = np.abs(blocks).max(-1, keepdims=True)
    byte = np.maximum(np.where(amax > 0, np.frexp(amax)[1] - 1 + 127, 0) - down, 1)
    scale = np.exp2(byte - 127.0)
    codes = (blocks / scale).astype(np.float32).astype(dtype).astype(np.float64)
    return np.moveaxis((codes * scale).reshape(v.shape), -1, axis)


WIDE = False


def mx_kscale(k):
    if not WIDE:
        return np.ones(k)
    levels = np.array([10, -10, 5, -5, 0])
    if k % 512:
        return np.exp2(np.random.permutation(np.resize(levels, k // 32))).repeat(32)
    a = np.empty((k // 512, 16))
    for p in range(k // 512):
        a[p, :8] = np.random.permutation(np.resize(levels, 8))
        for g in range(8):
            far = levels[np.abs(levels - a[p, g]) >= 10]
            a[p, g + 8] = far[np.random.randint(len(far))]
    return np.exp2(a.ravel()).repeat(32)


def f64(x):
    return np.asarray(x).astype(np.float64)


def striped(idx):
    return np.tile(idx.reshape(-1, 16).T, (8, 1)).astype(np.uint16)


def unstriped(offs):
    return offs[:16].T.reshape(-1).astype(np.int64)


E2M1 = np.array([0.0, 0.5, 1.0, 1.5, 2.0, 3.0, 4.0, 6.0, -0.0, -0.5, -1.0, -1.5, -2.0, -3.0, -4.0, -6.0])


def pack_weight(w, fmt):
    k, n = w.shape
    w = f64(np.asarray(w, np.float32).astype(ml_dtypes.bfloat16)).reshape(k // 32, 32, n)
    amax = np.abs(w).max(1)
    if fmt == "e4m3":
        byte = np.frexp(amax)[1] - 1 + 127 - 7
    else:
        mant, ex = np.frexp(amax / 6.0)
        byte = np.where(mant > 0.5, ex, ex - 1) + 127
    byte = np.clip(np.where(amax > 0, byte, 1), 1, 254)
    scaled = (w * np.exp2(127.0 - byte)[:, None, :]).reshape(k, n).astype(np.float32)
    by_word = np.ascontiguousarray(scaled.reshape(k // 512, 128, 4, n).transpose(0, 1, 3, 2))
    if fmt == "e4m3":
        words = by_word.astype(ml_dtypes.float8_e4m3fn).view(np.uint8)
    else:
        c = by_word.astype(ml_dtypes.float4_e2m1fn).view(np.uint8) & 0xF
        words = (c[..., 0::2] | (c[..., 1::2] << 4)).reshape(k // 512, 128, 2 * n)
    return np.ascontiguousarray(words), np.ascontiguousarray(byte.astype(np.uint8).reshape(k // 512, 16, n))


def unpack_weight(words, scales, fmt):
    g, _, n = scales.shape
    words = np.ascontiguousarray(words).reshape(g, 128, n, -1)
    if fmt == "e4m3":
        vals = words.view(ml_dtypes.float8_e4m3fn).astype(np.float64)
    else:
        nib = np.empty((g, 128, n, 4), np.uint8)
        nib[..., 0::2] = words & 0xF
        nib[..., 1::2] = words >> 4
        vals = E2M1[nib]
    vals = vals * np.repeat(np.exp2(scales.astype(np.float64) - 127.0), 8, axis=1)[..., None]
    return vals.transpose(0, 1, 3, 2).reshape(g * 512, n)


K, T, E, C, N = 1024, 640, 10, 128, 512
M = 256


def by_expert(wq, xq):
    return np.concatenate([wq[e].T @ xq[:, e * C:(e + 1) * C] for e in range(E)], axis=1)


def setup_inputs():
    n = np.random.standard_normal
    s = mx_kscale(K)[:, None]
    v = mx_kscale(N)
    first = np.random.permutation(np.repeat(np.arange(E), T // E))
    second = (first + 1 + np.random.permutation(np.repeat(np.arange(E - 1), -(-T // (E - 1)))[:T])) % E
    while np.bincount(second, minlength=E).max() != T // E:
        load = np.bincount(second, minlength=E); hi, lo = int(load.argmax()), int(load.argmin())
        t = np.flatnonzero((second == hi) & (first != lo))[0]; second[t] = lo
    slot_token = np.empty(E * C, np.int64); pos = np.empty((2, T), np.int64); fill = np.zeros(E, np.int64)
    place = np.stack([np.random.permutation(C) for _ in range(E)])
    for r, deal in enumerate((first, second)):
        for t in np.random.permutation(T):
            e = deal[t]; j = e * C + place[e, fill[e]]; fill[e] += 1; slot_token[j] = t; pos[r, t] = j
    g = np.random.uniform(0.2, 0.8, T)
    w = [pack_weight(m, "e2m1") for m in n((E, K, N)) / np.sqrt(K) / s[None] * v[None, None, :]]
    x = pack_weight(n((K, T)) * s, "e4m3")
    return {
        "x_words": x[0],
        "x_scales": x[1],
        "w_words": np.stack([m[0] for m in w]),
        "w_scales": np.stack([m[1] for m in w]),
        "b": (0.3 * n((N, E)) * v[:, None]).astype(np.float32),
        "wp": (n((N, M)) / np.sqrt(N) / v[:, None]).astype(np.float32),
        "gate": np.stack([np.tile(g, (N, 1)), np.tile(1.0 - g, (N, 1))]).astype(np.float32),
        "offs": striped(slot_token),
        "pos1": striped(pos[0]),
        "pos2": striped(pos[1]),
    }


def reference(x_words, x_scales, w_words, w_scales, b, wp, gate, offs, pos1, pos2):
    idx = unstriped(offs)
    w = np.stack([unpack_weight(w_words[e], w_scales[e], "e2m1") for e in range(E)])
    xq = unpack_weight(x_words, x_scales, "e4m3")[:, idx]
    y = by_expert(w, xq)
    y = y + np.repeat(f64(b), C, axis=1)
    c = f64(gate[0]) * y[:, unstriped(pos1)] + f64(gate[1]) * y[:, unstriped(pos2)]
    return mxq(f64(wp), 0, "e4m3").T @ mxq(c, 0, "e4m3")

@@ -1,0 +1,213 @@
+from contextlib import ExitStack
+
+import concourse.mybir as mybir
+from concourse.masks import make_identity
+
+K, T, E, C, N, M = 1024, 640, 10, 128, 512, 256
+S = E * C
+P = 128
+PASSES = K // 512
+NT = N // P
+
+FLOPS = 2 * S * K * N + 2 * T * N * M
+BYTES = K * T + K * T // 32 + E * K * N // 2 + E * K * N // 32 + 4 * (N * E + N * M + 2 * P * T + M * T) + 2 * P * (S + 2 * T) // 16
+
+F32 = mybir.dt.float32
+BF16 = mybir.dt.bfloat16
+I32 = mybir.dt.int32
+U32 = mybir.dt.uint32
+U16 = mybir.dt.uint16
+U8 = mybir.dt.uint8
+FP8X4 = mybir.dt.float8_e4m3fn_x4
+FP4X4 = mybir.dt.float4_e2m1fn_x4
+MULT = mybir.AluOpType.mult
+IDENTITY = mybir.ActivationFunctionType.Identity
+
+WORD_CUTS = (0, 384, 768, 1152, 1280)
+BYTE_CUTS = (0, 448, 896, 1280)
+TOKEN_CUTS = (0, 256, 512, 640)
+EARLY_TILES = 2
+BANK_EXPERTS = 4
+
+
+def spans(cuts):
+    return list(zip(cuts[:-1], cuts[1:]))
+
+
+def tile_moe_nxt_lin_bias_kernel(tc, x_words, x_scales, w_words, w_scales, b, wp, gate, offs, pos1, pos2, out):
+    nc = tc.nc
+    with ExitStack() as ctx:
+        keep = ctx.enter_context(tc.tile_pool(name="keep", bufs=1))
+        psum = ctx.enter_context(tc.psum_pool(name="psum", bufs=1))
+
+        offs_sb = keep.tile([P, S // 16], U16, name="offs_sb")
+        pos_sb = [keep.tile([P, T // 16], U16, name="pos_sb%d" % r) for r in range(2)]
+        x_bytes = keep.tile([P, T], U8, name="x_bytes", align_bytes=64)
+        x_sb = [keep.tile([P, T], I32, name="x_sb%d" % a, align_bytes=64) for a in range(PASSES)]
+        w_sb = [keep.tile([P, E * PASSES, 4 * P], U8, name="w_sb%d" % h, align_bytes=256) for h in range(2)]
+        w_plane = keep.tile([P, E * PASSES, N], U8, name="w_plane", align_bytes=256)
+        slot_words = [keep.tile([P, S], U32, name="slot_words%d" % a, align_bytes=64) for a in range(PASSES)]
+        slot_bytes = keep.tile([P, S], U8, name="slot_bytes", align_bytes=64)
+        moved_bytes = keep.tile([P, S], U8, name="moved_bytes", align_bytes=64)
+        b_sb = keep.tile([P, NT, E], F32, name="b_sb")
+        gate_sb = [keep.tile([P, T], F32, name="gate_sb%d" % r) for r in range(2)]
+        wp_raw = keep.tile([P, 4, M], F32, name="wp_raw")
+        ident = keep.tile([P, P], F32, name="ident")
+
+        nc.vector.memset(x_bytes[:].bitcast(I32), 0)
+        nc.vector.memset(w_plane[:].bitcast(I32), 0)
+        nc.vector.memset(moved_bytes[:].bitcast(I32), 0)
+        make_identity(nc, ident[:])
+
+        x_scale_words = x_scales.bitcast(I32)
+        w_by_half = w_words.bitcast(I32).rearrange("e a p (h c) -> h p (e a) c", h=2)
+        w_scale_rows = w_scales.bitcast(I32).rearrange("e a q c -> q (e a) c")
+
+        def load_w(h):
+            for g in range(2):
+                rows = slice(g * E, (g + 1) * E)
+                nc.sync.dma_start(w_sb[h][:, rows, :].bitcast(I32), w_by_half[h, :, rows, :])
+
+        nc.sync.dma_start(offs_sb[:], offs)
+        for q in range(4):
+            nc.sync.dma_start(x_bytes[32 * q : 32 * q + 8, :].bitcast(I32), x_scale_words[:, 4 * q : 4 * q + 4, :])
+        for a in range(PASSES):
+            nc.sync.dma_start(x_sb[a][:], x_words[a].rearrange("p t r -> p (t r)").bitcast(I32))
+        for q in range(4):
+            nc.sync.dma_start(w_plane[32 * q : 32 * q + 4].bitcast(I32), w_scale_rows[4 * q : 4 * q + 4])
+        load_w(0)
+        nc.sync.dma_start(b_sb[:], b.rearrange("(j p) e -> p j e", p=P))
+        nc.sync.dma_start(pos_sb[0][:], pos1)
+        nc.sync.dma_start(gate_sb[0][:], gate[0, 0:P, :])
+        nc.sync.dma_start(pos_sb[1][:], pos2)
+        nc.sync.dma_start(gate_sb[1][:], gate[1, 0:P, :])
+        nc.sync.dma_start(wp_raw[:], wp.rearrange("(p r) m -> p r m", r=4))
+        load_w(1)
+
+        for s0, s1 in spans(BYTE_CUTS):
+            nc.vector.tensor_copy(slot_bytes[:, s0:s1], x_bytes[:].indirect(offs_sb[:, s0 // 16 : s1 // 16]))
+        for q in range(4):
+            nc.scalar.dma_start(
+                moved_bytes[32 * q : 32 * q + 4, :].bitcast(I32), slot_bytes[32 * q + 4 : 32 * q + 8, :].bitcast(I32)
+            )
+        slot_plane = [slot_bytes, moved_bytes]
+        for s0, s1 in spans(WORD_CUTS):
+            for a in range(PASSES):
+                nc.vector.tensor_copy(
+                    slot_words[a][:, s0:s1], x_sb[a][:].bitcast(U32).indirect(offs_sb[:, s0 // 16 : s1 // 16])
+                )
+
+        y = [keep.tile([P, S], F32, name="y%d" % j) for j in range(NT)]
+
+        def experts(j):
+            half, word_bytes = j // 2, slice(2 * P * (j % 2), 2 * P * (j % 2 + 1))
+            for e0 in range(0, E, BANK_EXPERTS):
+                bank = psum.tile([P, BANK_EXPERTS * C], F32, name="bank", tag="mx", bufs=3)
+                group = range(e0, min(e0 + BANK_EXPERTS, E))
+                for e in group:
+                    slots = slice(e * C, (e + 1) * C)
+                    for a in range(PASSES):
+                        nc.tensor.matmul_mx(
+                            out=bank[:, (e - e0) * C : (e - e0 + 1) * C],
+                            lhsT=w_sb[half][:, e * PASSES + a, word_bytes].bitcast(FP4X4),
+                            lhsT_scale=w_plane[:, e * PASSES + a, j * P : (j + 1) * P],
+                            rhs=slot_words[a][:, slots].bitcast(FP8X4),
+                            rhs_scale=slot_plane[a][:, slots],
+                            start=(a == 0),
+                            stop=(a == PASSES - 1),
+                        )
+                for e in group:
+                    nc.scalar.activation(
+                        y[j][:, e * C : (e + 1) * C],
+                        bank[:, (e - e0) * C : (e - e0 + 1) * C],
+                        IDENTITY,
+                        bias=b_sb[:, j, e : e + 1],
+                    )
+
+        wp_grouped = keep.tile([P, M, 4], BF16, name="wp_grouped", align_bytes=64)
+        wp_codes = keep.tile([P, M], U32, name="wp_codes", align_bytes=64)
+        wp_plane = keep.tile([P, M], U8, name="wp_plane", align_bytes=64)
+
+        chunks = spans(TOKEN_CUTS)
+        c_turned = [
+            keep.tile([P, (t1 - t0) // P, 2, NT, 32, 2], BF16, name="c_turned%d" % t0, align_bytes=64) for t0, t1 in chunks
+        ]
+
+        def gated(j, t0, t1):
+            parts = []
+            for r in range(2):
+                part = keep.tile([P, t1 - t0], F32, name="part%d_%d_%d" % (j, t0, r))
+                nc.vector.tensor_tensor(
+                    part[:], y[j][:].indirect(pos_sb[r][:, t0 // 16 : t1 // 16]), gate_sb[r][:, t0:t1], MULT
+                )
+                parts.append(part)
+            return parts
+
+        def add_turned(j, i, parts, first):
+            t0, t1 = chunks[i]
+            blocks = (t1 - t0) // P
+            bank = psum.tile([P, blocks * P], F32, name="bank", tag="turn", bufs=5)
+            for r in range(2):
+                for k in range(blocks):
+                    c0 = t0 - first + k * P
+                    nc.tensor.matmul(
+                        bank[:, k * P : (k + 1) * P],
+                        lhsT=parts[r][:, c0 : c0 + P],
+                        rhs=ident[:],
+                        start=(r == 0 and k == 0),
+                        stop=(r == 1 and k == blocks - 1),
+                        is_transpose=True,
+                    )
+            nc.scalar.copy(
+                c_turned[i][:, :, :, j].rearrange("p k u q d -> p u k q d"),
+                bank[:].rearrange("p (k q u d) -> p u k q d", q=32, u=2, d=2),
+            )
+
+        def project(i):
+            t0, t1 = chunks[i]
+            width = t1 - t0
+            blocks = width // P
+            pairs = c_turned[i][:].rearrange("p k u j q d -> p (k u j q d)").bitcast(F32)
+            bank = psum.tile([P, blocks, 2, P], F32, name="bank", tag="turn", bufs=5)
+            for k in range(blocks):
+                for u in range(2):
+                    c0 = (2 * k + u) * P
+                    nc.tensor.transpose(bank[:, k, u, :], pairs[:, c0 : c0 + P], ident[:])
+            grouped = keep.tile([P, width * 4], BF16, name="grouped%d" % i, align_bytes=64)
+            nc.scalar.copy(
+                grouped[:].bitcast(F32).rearrange("p (k t u) -> p k t u", k=blocks, u=2),
+                bank[:].rearrange("p k u t -> p k t u"),
+            )
+            codes = keep.tile([P, width], U32, name="codes%d" % i, align_bytes=64)
+            plane = keep.tile([P, width], U8, name="plane%d" % i, align_bytes=64)
+            nc.vector.quantize_mx(out=codes[:].bitcast(FP8X4), scales=plane[:], in_=grouped[:])
+            sums = psum.tile([P, M // P, width], F32, name="bank", tag="mx", bufs=3)
+            for h in range(M // P):
+                nc.tensor.matmul_mx(
+                    out=sums[:, h, :],
+                    lhsT=wp_codes[:, h * P : (h + 1) * P].bitcast(FP8X4),
+                    lhsT_scale=wp_plane[:, h * P : (h + 1) * P],
+                    rhs=codes[:].bitcast(FP8X4),
+                    rhs_scale=plane[:],
+                    start=True,
+                    stop=True,
+                )
+            result = keep.tile([P, M // P, width], F32, name="result%d" % i)
+            nc.scalar.copy(result[:], sums[:])
+            nc.sync.dma_start(out.rearrange("(h p) t -> p h t", p=P)[:, :, t0:t1], result[:])
+
+        experts(0)
+        nc.vector.tensor_copy(wp_grouped[:], wp_raw[:].rearrange("p r m -> p m r"))
+        nc.vector.quantize_mx(
+            out=wp_codes[:].bitcast(FP8X4), scales=wp_plane[:], in_=wp_grouped[:].rearrange("p m r -> p (m r)")
+        )
+        experts(1)
+        for j in range(EARLY_TILES):
+            parts = gated(j, 0, T)
+            experts(j + 2)
+            for i in range(len(chunks)):
+                add_turned(j, i, parts, 0)
+        for i, (t0, t1) in enumerate(chunks):
+            for j in range(EARLY_TILES, NT):
+                add_turned(j, i, gated(j, t0, t1), t0)
+            project(i)

@@ -26,8 +26,9 @@ IDENTITY = mybir.ActivationFunctionType.Identity
 WORD_CUTS = (0, 384, 768, 1152, 1280)
 BYTE_CUTS = (0, 448, 896, 1280)
 TOKEN_CUTS = (0, 256, 512, 640)
-EARLY_TILES = 2
-BANK_EXPERTS = 4
+BANK_CUTS = (0, 512, 640)
+BANK_BYTES = 2048
+HALF_BYTES = E * PASSES * 4 * P
 
 
 def spans(cuts):
@@ -38,24 +39,24 @@ def tile_moe_nxt_lin_bias_kernel(tc, x_words, x_scales, w_words, w_scales, b, wp
     nc = tc.nc
     with ExitStack() as ctx:
         keep = ctx.enter_context(tc.tile_pool(name="keep", bufs=1))
+        early = ctx.enter_context(tc.tile_pool(name="early", bufs=1))
         psum = ctx.enter_context(tc.psum_pool(name="psum", bufs=1))
 
         offs_sb = keep.tile([P, S // 16], U16, name="offs_sb")
         pos_sb = [keep.tile([P, T // 16], U16, name="pos_sb%d" % r) for r in range(2)]
-        x_bytes = keep.tile([P, T], U8, name="x_bytes", align_bytes=64)
-        x_sb = [keep.tile([P, T], I32, name="x_sb%d" % a, align_bytes=64) for a in range(PASSES)]
-        w_sb = [keep.tile([P, E * PASSES, 4 * P], U8, name="w_sb%d" % h, align_bytes=256) for h in range(2)]
+        x_bytes = early.tile([P, T], U8, name="x_bytes", align_bytes=256, offset=HALF_BYTES - 256)
+        x_sb = keep.tile([P, PASSES, T], I32, name="x_sb", tag="second", align_bytes=64)
+        w_sb = [keep.tile([P, E * PASSES, 4 * P], U8, name="w_sb0", align_bytes=256)]
         w_plane = keep.tile([P, E * PASSES, N], U8, name="w_plane", align_bytes=256)
         slot_words = [keep.tile([P, S], U32, name="slot_words%d" % a, align_bytes=64) for a in range(PASSES)]
         slot_bytes = keep.tile([P, S], U8, name="slot_bytes", align_bytes=64)
         moved_bytes = keep.tile([P, S], U8, name="moved_bytes", align_bytes=64)
         b_sb = keep.tile([P, NT, E], F32, name="b_sb")
-        gate_sb = [keep.tile([P, T], F32, name="gate_sb%d" % r) for r in range(2)]
-        wp_raw = keep.tile([P, 4, M], F32, name="wp_raw")
         ident = keep.tile([P, P], F32, name="ident")
 
-        nc.vector.memset(x_bytes[:].bitcast(I32), 0)
-        nc.vector.memset(w_plane[:].bitcast(I32), 0)
+        nc.gpsimd.memset(x_bytes[:].bitcast(I32), 0)
+        nc.vector.memset(w_plane[:, 0:E, :].bitcast(I32), 0)
+        nc.gpsimd.memset(w_plane[:, E : 2 * E, :].bitcast(I32), 0)
         nc.vector.memset(moved_bytes[:].bitcast(I32), 0)
         make_identity(nc, ident[:])
 
@@ -63,26 +64,17 @@ def tile_moe_nxt_lin_bias_kernel(tc, x_words, x_scales, w_words, w_scales, b, wp
         w_by_half = w_words.bitcast(I32).rearrange("e a p (h c) -> h p (e a) c", h=2)
         w_scale_rows = w_scales.bitcast(I32).rearrange("e a q c -> q (e a) c")
 
-        def load_w(h):
-            for g in range(2):
-                rows = slice(g * E, (g + 1) * E)
-                nc.sync.dma_start(w_sb[h][:, rows, :].bitcast(I32), w_by_half[h, :, rows, :])
-
         nc.sync.dma_start(offs_sb[:], offs)
         for q in range(4):
             nc.sync.dma_start(x_bytes[32 * q : 32 * q + 8, :].bitcast(I32), x_scale_words[:, 4 * q : 4 * q + 4, :])
-        for a in range(PASSES):
-            nc.sync.dma_start(x_sb[a][:], x_words[a].rearrange("p t r -> p (t r)").bitcast(I32))
-        for q in range(4):
-            nc.sync.dma_start(w_plane[32 * q : 32 * q + 4].bitcast(I32), w_scale_rows[4 * q : 4 * q + 4])
-        load_w(0)
-        nc.sync.dma_start(b_sb[:], b.rearrange("(j p) e -> p j e", p=P))
+        nc.sync.dma_start(x_sb[:], x_words.rearrange("a p t r -> p a (t r)").bitcast(I32))
         nc.sync.dma_start(pos_sb[0][:], pos1)
-        nc.sync.dma_start(gate_sb[0][:], gate[0, 0:P, :])
         nc.sync.dma_start(pos_sb[1][:], pos2)
-        nc.sync.dma_start(gate_sb[1][:], gate[1, 0:P, :])
-        nc.sync.dma_start(wp_raw[:], wp.rearrange("(p r) m -> p r m", r=4))
-        load_w(1)
+        nc.sync.dma_start(b_sb[:], b.rearrange("(j p) e -> p j e", p=P))
+        nc.sync.dma_start(w_sb[0][:].bitcast(I32), w_by_half[0])
+        for q in range(4):
+            queue = nc.scalar if q < 2 else nc.sync
+            queue.dma_start(w_plane[32 * q : 32 * q + 4].bitcast(I32), w_scale_rows[4 * q : 4 * q + 4])
 
         for s0, s1 in spans(BYTE_CUTS):
             nc.vector.tensor_copy(slot_bytes[:, s0:s1], x_bytes[:].indirect(offs_sb[:, s0 // 16 : s1 // 16]))
@@ -91,19 +83,29 @@ def tile_moe_nxt_lin_bias_kernel(tc, x_words, x_scales, w_words, w_scales, b, wp
                 moved_bytes[32 * q : 32 * q + 4, :].bitcast(I32), slot_bytes[32 * q + 4 : 32 * q + 8, :].bitcast(I32)
             )
         slot_plane = [slot_bytes, moved_bytes]
+        gate_sb = early.tile([P, 2, T], F32, name="gate_sb", align_bytes=256, offset=HALF_BYTES)
+        nc.sync.dma_start(gate_sb[:], gate[:, 0:P, :].rearrange("r p t -> p r t"))
+        w_sb.append(early.tile([P, E * PASSES, 4 * P], U8, name="w_sb1", align_bytes=256, offset=0))
+        nc.sync.dma_start(w_sb[1][:].bitcast(I32), w_by_half[1])
         for s0, s1 in spans(WORD_CUTS):
             for a in range(PASSES):
                 nc.vector.tensor_copy(
-                    slot_words[a][:, s0:s1], x_sb[a][:].bitcast(U32).indirect(offs_sb[:, s0 // 16 : s1 // 16])
+                    slot_words[a][:, s0:s1], x_sb[:, a, :].bitcast(U32).indirect(offs_sb[:, s0 // 16 : s1 // 16])
                 )
+
+        wp_raw = keep.tile([P, 4, M], F32, name="wp_raw", tag="second", align_bytes=64)
+        nc.sync.dma_start(wp_raw[:], wp.rearrange("(p r) m -> p r m", r=4))
 
         y = [keep.tile([P, S], F32, name="y%d" % j) for j in range(NT)]
 
-        def experts(j):
+        def bank_tile(shape, number):
+            return psum.tile(shape, F32, name="bank", offset=number * BANK_BYTES)
+
+        def experts(j, cuts, banks):
             half, word_bytes = j // 2, slice(2 * P * (j % 2), 2 * P * (j % 2 + 1))
-            for e0 in range(0, E, BANK_EXPERTS):
-                bank = psum.tile([P, BANK_EXPERTS * C], F32, name="bank", tag="mx", bufs=3)
-                group = range(e0, min(e0 + BANK_EXPERTS, E))
+            for (e0, e1), number in zip(spans(cuts), banks):
+                bank = bank_tile([P, (e1 - e0) * C], number)
+                group = range(e0, e1)
                 for e in group:
                     slots = slice(e * C, (e + 1) * C)
                     for a in range(PASSES):
@@ -124,29 +126,25 @@ def tile_moe_nxt_lin_bias_kernel(tc, x_words, x_scales, w_words, w_scales, b, wp
                         bias=b_sb[:, j, e : e + 1],
                     )
 
-        wp_grouped = keep.tile([P, M, 4], BF16, name="wp_grouped", align_bytes=64)
         wp_codes = keep.tile([P, M], U32, name="wp_codes", align_bytes=64)
         wp_plane = keep.tile([P, M], U8, name="wp_plane", align_bytes=64)
 
         chunks = spans(TOKEN_CUTS)
-        c_turned = [
-            keep.tile([P, (t1 - t0) // P, 2, NT, 32, 2], BF16, name="c_turned%d" % t0, align_bytes=64) for t0, t1 in chunks
-        ]
+        c_turned = keep.tile([P, T // P, 2, NT, 32, 2], BF16, name="c_turned", align_bytes=64)
 
         def gated(j, t0, t1):
             parts = []
             for r in range(2):
-                part = keep.tile([P, t1 - t0], F32, name="part%d_%d_%d" % (j, t0, r))
+                part = keep.tile([P, t1 - t0], F32, name="part%d_%d_%d" % (j, t0, r), align_bytes=64)
                 nc.vector.tensor_tensor(
-                    part[:], y[j][:].indirect(pos_sb[r][:, t0 // 16 : t1 // 16]), gate_sb[r][:, t0:t1], MULT
+                    part[:], y[j][:].indirect(pos_sb[r][:, t0 // 16 : t1 // 16]), gate_sb[:, r, t0:t1], MULT
                 )
                 parts.append(part)
             return parts
 
-        def add_turned(j, i, parts, first):
-            t0, t1 = chunks[i]
+        def add_turned(j, t0, t1, parts, first, number):
             blocks = (t1 - t0) // P
-            bank = psum.tile([P, blocks * P], F32, name="bank", tag="turn", bufs=5)
+            bank = bank_tile([P, blocks * P], number)
             for r in range(2):
                 for k in range(blocks):
                     c0 = t0 - first + k * P
@@ -159,29 +157,35 @@ def tile_moe_nxt_lin_bias_kernel(tc, x_words, x_scales, w_words, w_scales, b, wp
                         is_transpose=True,
                     )
             nc.scalar.copy(
-                c_turned[i][:, :, :, j].rearrange("p k u q d -> p u k q d"),
+                c_turned[:, t0 // P : t1 // P, :, j].rearrange("p k u q d -> p u k q d"),
                 bank[:].rearrange("p (k q u d) -> p u k q d", q=32, u=2, d=2),
             )
 
-        def project(i):
+        def turn_back(i, number, on_vector):
             t0, t1 = chunks[i]
             width = t1 - t0
             blocks = width // P
-            pairs = c_turned[i][:].rearrange("p k u j q d -> p (k u j q d)").bitcast(F32)
-            bank = psum.tile([P, blocks, 2, P], F32, name="bank", tag="turn", bufs=5)
+            pairs = c_turned[:, t0 // P : t1 // P].rearrange("p k u j q d -> p (k u j q d)").bitcast(F32)
+            bank = bank_tile([P, blocks, 2, P], number)
             for k in range(blocks):
                 for u in range(2):
                     c0 = (2 * k + u) * P
                     nc.tensor.transpose(bank[:, k, u, :], pairs[:, c0 : c0 + P], ident[:])
             grouped = keep.tile([P, width * 4], BF16, name="grouped%d" % i, align_bytes=64)
-            nc.scalar.copy(
+            copy_out = nc.vector.tensor_copy if on_vector else nc.scalar.copy
+            copy_out(
                 grouped[:].bitcast(F32).rearrange("p (k t u) -> p k t u", k=blocks, u=2),
                 bank[:].rearrange("p k u t -> p k t u"),
             )
+            return grouped
+
+        def project(i, grouped, number):
+            t0, t1 = chunks[i]
+            width = t1 - t0
             codes = keep.tile([P, width], U32, name="codes%d" % i, align_bytes=64)
             plane = keep.tile([P, width], U8, name="plane%d" % i, align_bytes=64)
             nc.vector.quantize_mx(out=codes[:].bitcast(FP8X4), scales=plane[:], in_=grouped[:])
-            sums = psum.tile([P, M // P, width], F32, name="bank", tag="mx", bufs=3)
+            sums = bank_tile([P, M // P, width], number)
             for h in range(M // P):
                 nc.tensor.matmul_mx(
                     out=sums[:, h, :],
@@ -192,22 +196,37 @@ def tile_moe_nxt_lin_bias_kernel(tc, x_words, x_scales, w_words, w_scales, b, wp
                     start=True,
                     stop=True,
                 )
-            result = keep.tile([P, M // P, width], F32, name="result%d" % i)
-            nc.scalar.copy(result[:], sums[:])
+            return sums
+
+        def store(i, sums, on_vector):
+            t0, t1 = chunks[i]
+            result = keep.tile([P, M // P, t1 - t0], F32, name="result%d" % i)
+            if on_vector:
+                nc.vector.tensor_copy(result[:], sums[:])
+            else:
+                nc.scalar.copy(result[:], sums[:])
             nc.sync.dma_start(out.rearrange("(h p) t -> p h t", p=P)[:, :, t0:t1], result[:])
 
-        experts(0)
-        nc.vector.tensor_copy(wp_grouped[:], wp_raw[:].rearrange("p r m -> p m r"))
-        nc.vector.quantize_mx(
-            out=wp_codes[:].bitcast(FP8X4), scales=wp_plane[:], in_=wp_grouped[:].rearrange("p m r -> p (m r)")
-        )
-        experts(1)
-        for j in range(EARLY_TILES):
-            parts = gated(j, 0, T)
-            experts(j + 2)
-            for i in range(len(chunks)):
-                add_turned(j, i, parts, 0)
+        experts(0, (0, 3, 6, 9, 10), (0, 1, 2, 6))
+        experts(1, (0, 4, 8, 10), (3, 4, 5))
+        early_parts = [gated(0, 0, T)]
+        experts(2, (0, 4, 8, 10), (0, 1, 2))
+        early_parts.append(gated(1, 0, T))
+        experts(3, (0, 4, 8, 10), (3, 4, 5))
+        early_parts.append(gated(2, 0, T))
+        for j, banks in enumerate(((1, 2), (4, 5), (1, 2))):
+            for (t0, t1), number in zip(spans(BANK_CUTS), banks):
+                add_turned(j, t0, t1, early_parts[j], 0, number)
+            if j == 0:
+                wp_grouped = keep.tile([P, M, 4], BF16, name="wp_grouped", tag="part0_0_1", align_bytes=64)
+                nc.scalar.copy(wp_grouped[:], wp_raw[:].rearrange("p r m -> p m r"))
+                nc.vector.quantize_mx(
+                    out=wp_codes[:].bitcast(FP8X4), scales=wp_plane[:], in_=wp_grouped[:].rearrange("p m r -> p (m r)")
+                )
+        grouped = []
         for i, (t0, t1) in enumerate(chunks):
-            for j in range(EARLY_TILES, NT):
-                add_turned(j, i, gated(j, t0, t1), t0)
-            project(i)
+            add_turned(NT - 1, t0, t1, gated(NT - 1, t0, t1), t0, 6)
+            grouped.append(turn_back(i, (7, 0, 3)[i], i == 1))
+        sums = [project(i, grouped[i], (6, 3, 4)[i]) for i in range(len(chunks))]
+        for i in range(len(chunks)):
+            store(i, sums[i], i == 1)

@@ -28,7 +28,6 @@ BYTE_CUTS = (0, 448, 896, 1280)
 TOKEN_CUTS = (0, 256, 512, 640)
 BANK_CUTS = (0, 512, 640)
 BANK_BYTES = 2048
-HALF_BYTES = E * PASSES * 4 * P
 
 
 def spans(cuts):
@@ -39,14 +38,13 @@ def tile_moe_nxt_lin_bias_kernel(tc, x_words, x_scales, w_words, w_scales, b, wp
     nc = tc.nc
     with ExitStack() as ctx:
         keep = ctx.enter_context(tc.tile_pool(name="keep", bufs=1))
-        early = ctx.enter_context(tc.tile_pool(name="early", bufs=1))
         psum = ctx.enter_context(tc.psum_pool(name="psum", bufs=1))
 
         offs_sb = keep.tile([P, S // 16], U16, name="offs_sb")
         pos_sb = [keep.tile([P, T // 16], U16, name="pos_sb%d" % r) for r in range(2)]
-        x_bytes = early.tile([P, T], U8, name="x_bytes", align_bytes=256, offset=HALF_BYTES - 256)
-        x_sb = keep.tile([P, PASSES, T], I32, name="x_sb", tag="second", align_bytes=64)
-        w_sb = [keep.tile([P, E * PASSES, 4 * P], U8, name="w_sb0", align_bytes=256)]
+        x_bytes = keep.tile([P, T], U8, name="x_bytes", align_bytes=64)
+        x_sb = keep.tile([P, PASSES, T], I32, name="x_sb", align_bytes=64)
+        w_sb = [keep.tile([P, E * PASSES, 4 * P], U8, name="w_sb%d" % h, align_bytes=256) for h in range(2)]
         w_plane = keep.tile([P, E * PASSES, N], U8, name="w_plane", align_bytes=256)
         slot_words = [keep.tile([P, S], U32, name="slot_words%d" % a, align_bytes=64) for a in range(PASSES)]
         slot_bytes = keep.tile([P, S], U8, name="slot_bytes", align_bytes=64)
@@ -62,39 +60,34 @@ def tile_moe_nxt_lin_bias_kernel(tc, x_words, x_scales, w_words, w_scales, b, wp
 
         x_scale_words = x_scales.bitcast(I32)
         w_by_half = w_words.bitcast(I32).rearrange("e a p (h c) -> h p (e a) c", h=2)
-        w_scale_rows = w_scales.bitcast(I32).rearrange("e a q c -> q (e a) c")
+        w_scale_rows = w_scales.bitcast(I32).rearrange("e a (q r) c -> r q (e a) c", r=4)
 
         nc.sync.dma_start(offs_sb[:], offs)
+        nc.scalar.dma_start(b_sb[:], b.rearrange("(j p) e -> p j e", p=P))
         for q in range(4):
             nc.sync.dma_start(x_bytes[32 * q : 32 * q + 8, :].bitcast(I32), x_scale_words[:, 4 * q : 4 * q + 4, :])
         nc.sync.dma_start(x_sb[:], x_words.rearrange("a p t r -> p a (t r)").bitcast(I32))
         nc.sync.dma_start(pos_sb[0][:], pos1)
         nc.sync.dma_start(pos_sb[1][:], pos2)
-        nc.sync.dma_start(b_sb[:], b.rearrange("(j p) e -> p j e", p=P))
         nc.sync.dma_start(w_sb[0][:].bitcast(I32), w_by_half[0])
-        for q in range(4):
-            queue = nc.scalar if q < 2 else nc.sync
-            queue.dma_start(w_plane[32 * q : 32 * q + 4].bitcast(I32), w_scale_rows[4 * q : 4 * q + 4])
+        for r in range(4):
+            nc.scalar.dma_start(w_plane[r:P:32].bitcast(I32), w_scale_rows[r])
 
         for s0, s1 in spans(BYTE_CUTS):
             nc.vector.tensor_copy(slot_bytes[:, s0:s1], x_bytes[:].indirect(offs_sb[:, s0 // 16 : s1 // 16]))
-        for q in range(4):
-            nc.scalar.dma_start(
-                moved_bytes[32 * q : 32 * q + 4, :].bitcast(I32), slot_bytes[32 * q + 4 : 32 * q + 8, :].bitcast(I32)
-            )
+        for r in range(4):
+            nc.sync.dma_start(moved_bytes[r:P:32, :].bitcast(I32), slot_bytes[4 + r : P : 32, :].bitcast(I32))
         slot_plane = [slot_bytes, moved_bytes]
-        gate_sb = early.tile([P, 2, T], F32, name="gate_sb", align_bytes=256, offset=HALF_BYTES)
+        gate_sb = keep.tile([P, 2, T], F32, name="gate_sb")
         nc.sync.dma_start(gate_sb[:], gate[:, 0:P, :].rearrange("r p t -> p r t"))
-        w_sb.append(early.tile([P, E * PASSES, 4 * P], U8, name="w_sb1", align_bytes=256, offset=0))
         nc.sync.dma_start(w_sb[1][:].bitcast(I32), w_by_half[1])
+        wp_raw = keep.tile([P, 4, M], F32, name="wp_raw")
+        nc.sync.dma_start(wp_raw[:], wp.rearrange("(p r) m -> p r m", r=4))
         for s0, s1 in spans(WORD_CUTS):
             for a in range(PASSES):
                 nc.vector.tensor_copy(
                     slot_words[a][:, s0:s1], x_sb[:, a, :].bitcast(U32).indirect(offs_sb[:, s0 // 16 : s1 // 16])
                 )
-
-        wp_raw = keep.tile([P, 4, M], F32, name="wp_raw", tag="second", align_bytes=64)
-        nc.sync.dma_start(wp_raw[:], wp.rearrange("(p r) m -> p r m", r=4))
 
         y = [keep.tile([P, S], F32, name="y%d" % j) for j in range(NT)]
 
@@ -132,14 +125,12 @@ def tile_moe_nxt_lin_bias_kernel(tc, x_words, x_scales, w_words, w_scales, b, wp
         chunks = spans(TOKEN_CUTS)
         c_turned = keep.tile([P, T // P, 2, NT, 32, 2], BF16, name="c_turned", align_bytes=64)
 
-        def gated(j, t0, t1):
-            parts = []
+        def gated(j, t0, t1, tag):
+            parts = keep.tile([P, 2, t1 - t0], F32, name="parts", tag=tag, align_bytes=64)
             for r in range(2):
-                part = keep.tile([P, t1 - t0], F32, name="part%d_%d_%d" % (j, t0, r), align_bytes=64)
                 nc.vector.tensor_tensor(
-                    part[:], y[j][:].indirect(pos_sb[r][:, t0 // 16 : t1 // 16]), gate_sb[:, r, t0:t1], MULT
+                    parts[:, r, :], y[j][:].indirect(pos_sb[r][:, t0 // 16 : t1 // 16]), gate_sb[:, r, t0:t1], MULT
                 )
-                parts.append(part)
             return parts
 
         def add_turned(j, t0, t1, parts, first, number):
@@ -150,7 +141,7 @@ def tile_moe_nxt_lin_bias_kernel(tc, x_words, x_scales, w_words, w_scales, b, wp
                     c0 = t0 - first + k * P
                     nc.tensor.matmul(
                         bank[:, k * P : (k + 1) * P],
-                        lhsT=parts[r][:, c0 : c0 + P],
+                        lhsT=parts[:, r, c0 : c0 + P],
                         rhs=ident[:],
                         start=(r == 0 and k == 0),
                         stop=(r == 1 and k == blocks - 1),
@@ -209,24 +200,24 @@ def tile_moe_nxt_lin_bias_kernel(tc, x_words, x_scales, w_words, w_scales, b, wp
 
         experts(0, (0, 3, 6, 9, 10), (0, 1, 2, 6))
         experts(1, (0, 4, 8, 10), (3, 4, 5))
-        early_parts = [gated(0, 0, T)]
+        early_parts = [gated(0, 0, T, "parts0")]
         experts(2, (0, 4, 8, 10), (0, 1, 2))
-        early_parts.append(gated(1, 0, T))
+        early_parts.append(gated(1, 0, T, "parts1"))
         experts(3, (0, 4, 8, 10), (3, 4, 5))
-        early_parts.append(gated(2, 0, T))
-        for j, banks in enumerate(((1, 2), (4, 5), (1, 2))):
+        for j, banks in enumerate(((1, 2), (4, 5))):
             for (t0, t1), number in zip(spans(BANK_CUTS), banks):
                 add_turned(j, t0, t1, early_parts[j], 0, number)
             if j == 0:
-                wp_grouped = keep.tile([P, M, 4], BF16, name="wp_grouped", tag="part0_0_1", align_bytes=64)
+                wp_grouped = keep.tile([P, M, 4], BF16, name="wp_grouped", tag="parts0", align_bytes=64)
                 nc.scalar.copy(wp_grouped[:], wp_raw[:].rearrange("p r m -> p m r"))
                 nc.vector.quantize_mx(
                     out=wp_codes[:].bitcast(FP8X4), scales=wp_plane[:], in_=wp_grouped[:].rearrange("p m r -> p (m r)")
                 )
         grouped = []
         for i, (t0, t1) in enumerate(chunks):
-            add_turned(NT - 1, t0, t1, gated(NT - 1, t0, t1), t0, 6)
-            grouped.append(turn_back(i, (7, 0, 3)[i], i == 1))
-        sums = [project(i, grouped[i], (6, 3, 4)[i]) for i in range(len(chunks))]
+            add_turned(2, t0, t1, gated(2, t0, t1, "parts2"), t0, (1, 2, 7)[i])
+            add_turned(3, t0, t1, gated(3, t0, t1, "parts3_%d" % i), t0, 0)
+            grouped.append(turn_back(i, (7, 3, 4)[i], i == 1))
+        sums = [project(i, grouped[i], (0, 4, 5)[i]) for i in range(len(chunks))]
         for i in range(len(chunks)):
             store(i, sums[i], i == 1)

@@ -38,6 +38,7 @@ def tile_moe_nxt_lin_bias_kernel(tc, x_words, x_scales, w_words, w_scales, b, wp
     nc = tc.nc
     with ExitStack() as ctx:
         keep = ctx.enter_context(tc.tile_pool(name="keep", bufs=1))
+        late = ctx.enter_context(tc.tile_pool(name="late", bufs=1))
         psum = ctx.enter_context(tc.psum_pool(name="psum", bufs=1))
 
         offs_sb = keep.tile([P, S // 16], U16, name="offs_sb")
@@ -49,7 +50,7 @@ def tile_moe_nxt_lin_bias_kernel(tc, x_words, x_scales, w_words, w_scales, b, wp
         slot_words = [keep.tile([P, S], U32, name="slot_words%d" % a, align_bytes=64) for a in range(PASSES)]
         slot_bytes = keep.tile([P, S], U8, name="slot_bytes", align_bytes=64)
         moved_bytes = keep.tile([P, S], U8, name="moved_bytes", align_bytes=64)
-        b_sb = keep.tile([P, NT, E], F32, name="b_sb")
+        b_sb = late.tile([P, NT, 16], F32, name="b_sb", offset=2048 - 64)
         ident = keep.tile([P, P], F32, name="ident")
 
         nc.gpsimd.memset(x_bytes[:].bitcast(I32), 0)
@@ -63,7 +64,7 @@ def tile_moe_nxt_lin_bias_kernel(tc, x_words, x_scales, w_words, w_scales, b, wp
         w_scale_rows = w_scales.bitcast(I32).rearrange("e a (q r) c -> r q (e a) c", r=4)
 
         nc.sync.dma_start(offs_sb[:], offs)
-        nc.scalar.dma_start(b_sb[:], b.rearrange("(j p) e -> p j e", p=P))
+        nc.scalar.dma_start(b_sb[:, :, 0:E], b.rearrange("(j p) e -> p j e", p=P))
         for q in range(4):
             nc.sync.dma_start(x_bytes[32 * q : 32 * q + 8, :].bitcast(I32), x_scale_words[:, 4 * q : 4 * q + 4, :])
         nc.sync.dma_start(x_sb[:], x_words.rearrange("a p t r -> p a (t r)").bitcast(I32))
@@ -94,7 +95,7 @@ def tile_moe_nxt_lin_bias_kernel(tc, x_words, x_scales, w_words, w_scales, b, wp
         def bank_tile(shape, number):
             return psum.tile(shape, F32, name="bank", offset=number * BANK_BYTES)
 
-        def experts(j, cuts, banks):
+        def experts(j, cuts, banks, on_vector=False):
             half, word_bytes = j // 2, slice(2 * P * (j % 2), 2 * P * (j % 2 + 1))
             for (e0, e1), number in zip(spans(cuts), banks):
                 bank = bank_tile([P, (e1 - e0) * C], number)
@@ -112,12 +113,12 @@ def tile_moe_nxt_lin_bias_kernel(tc, x_words, x_scales, w_words, w_scales, b, wp
                             stop=(a == PASSES - 1),
                         )
                 for e in group:
-                    nc.scalar.activation(
-                        y[j][:, e * C : (e + 1) * C],
-                        bank[:, (e - e0) * C : (e - e0 + 1) * C],
-                        IDENTITY,
-                        bias=b_sb[:, j, e : e + 1],
-                    )
+                    slots = slice(e * C, (e + 1) * C)
+                    sums = bank[:, (e - e0) * C : (e - e0 + 1) * C]
+                    if on_vector:
+                        nc.vector.tensor_scalar_add(y[j][:, slots], sums, b_sb[:, j, e : e + 1])
+                    else:
+                        nc.scalar.activation(y[j][:, slots], sums, IDENTITY, bias=b_sb[:, j, e : e + 1])
 
         wp_codes = keep.tile([P, M], U32, name="wp_codes", align_bytes=64)
         wp_plane = keep.tile([P, M], U8, name="wp_plane", align_bytes=64)
@@ -125,8 +126,7 @@ def tile_moe_nxt_lin_bias_kernel(tc, x_words, x_scales, w_words, w_scales, b, wp
         chunks = spans(TOKEN_CUTS)
         c_turned = keep.tile([P, T // P, 2, NT, 32, 2], BF16, name="c_turned", align_bytes=64)
 
-        def gated(j, t0, t1, tag):
-            parts = keep.tile([P, 2, t1 - t0], F32, name="parts", tag=tag, align_bytes=64)
+        def gated(j, t0, t1, parts):
             for r in range(2):
                 nc.vector.tensor_tensor(
                     parts[:, r, :], y[j][:].indirect(pos_sb[r][:, t0 // 16 : t1 // 16]), gate_sb[:, r, t0:t1], MULT
@@ -198,13 +198,19 @@ def tile_moe_nxt_lin_bias_kernel(tc, x_words, x_scales, w_words, w_scales, b, wp
                 nc.scalar.copy(result[:], sums[:])
             nc.sync.dma_start(out.rearrange("(h p) t -> p h t", p=P)[:, :, t0:t1], result[:])
 
-        experts(0, (0, 3, 6, 9, 10), (0, 1, 2, 6))
-        experts(1, (0, 4, 8, 10), (3, 4, 5))
-        early_parts = [gated(0, 0, T, "parts0")]
+        def parts_tile(name, width):
+            return keep.tile([P, 2, width], F32, name=name, align_bytes=64)
+
+        experts(0, (0, 3, 6), (0, 1))
+        experts(1, (0, 3, 6), (3, 4))
+        experts(0, (6, 9), (2,))
+        experts(0, (9, 10), (6,), on_vector=True)
+        experts(1, (6, 10), (5,))
+        early_parts = [gated(0, 0, T, parts_tile("parts0", T))]
         experts(2, (0, 4, 8, 10), (0, 1, 2))
-        early_parts.append(gated(1, 0, T, "parts1"))
+        early_parts.append(gated(1, 0, T, parts_tile("parts1", T)))
         experts(3, (0, 4, 8, 10), (3, 4, 5))
-        for j, banks in enumerate(((1, 2), (4, 5))):
+        for j, banks in enumerate(((1, 2), (3, 4))):
             for (t0, t1), number in zip(spans(BANK_CUTS), banks):
                 add_turned(j, t0, t1, early_parts[j], 0, number)
             if j == 0:
@@ -215,9 +221,13 @@ def tile_moe_nxt_lin_bias_kernel(tc, x_words, x_scales, w_words, w_scales, b, wp
                 )
         grouped = []
         for i, (t0, t1) in enumerate(chunks):
-            add_turned(2, t0, t1, gated(2, t0, t1, "parts2"), t0, (1, 2, 7)[i])
-            add_turned(3, t0, t1, gated(3, t0, t1, "parts3_%d" % i), t0, 0)
-            grouped.append(turn_back(i, (7, 3, 4)[i], i == 1))
-        sums = [project(i, grouped[i], (0, 4, 5)[i]) for i in range(len(chunks))]
+            if i == 0:
+                parts = parts_tile("parts2", t1 - t0)
+            else:
+                parts = late.tile([P, 2, t1 - t0], F32, name="parts2_%d" % i, offset=2048 * (i - 1))
+            add_turned(2, t0, t1, gated(2, t0, t1, parts), t0, (5, 6, 7)[i])
+            add_turned(3, t0, t1, gated(3, t0, t1, parts_tile("parts3_%d" % i, t1 - t0)), t0, 0)
+            grouped.append(turn_back(i, (7, 1, 2)[i], i == 1))
+        sums = [project(i, grouped[i], (7, 4, 3)[i]) for i in range(len(chunks))]
         for i in range(len(chunks)):
-            store(i, sums[i], i == 1)
+            store(i, sums[i], i != 1)

@@ -46,7 +46,7 @@ def tile_moe_nxt_lin_bias_kernel(tc, x_words, x_scales, w_words, w_scales, b, wp
         x_bytes = keep.tile([P, T], U8, name="x_bytes", align_bytes=64)
         x_sb = keep.tile([P, PASSES, T], I32, name="x_sb", align_bytes=64)
         w_sb = [keep.tile([P, E * PASSES, 4 * P], U8, name="w_sb%d" % h, align_bytes=256) for h in range(2)]
-        w_plane = keep.tile([P, E * PASSES, N], U8, name="w_plane", align_bytes=256)
+        w_plane = [keep.tile([P, E * PASSES, 2 * P], U8, name="w_plane%d" % h, align_bytes=256) for h in range(2)]
         slot_words = [keep.tile([P, S], U32, name="slot_words%d" % a, align_bytes=64) for a in range(PASSES)]
         slot_bytes = keep.tile([P, S], U8, name="slot_bytes", align_bytes=64)
         moved_bytes = keep.tile([P, S], U8, name="moved_bytes", align_bytes=64)
@@ -54,14 +54,14 @@ def tile_moe_nxt_lin_bias_kernel(tc, x_words, x_scales, w_words, w_scales, b, wp
         ident = keep.tile([P, P], F32, name="ident")
 
         nc.gpsimd.memset(x_bytes[:].bitcast(I32), 0)
-        nc.vector.memset(w_plane[:, 0:E, :].bitcast(I32), 0)
-        nc.gpsimd.memset(w_plane[:, E : 2 * E, :].bitcast(I32), 0)
+        nc.vector.memset(w_plane[0][:].bitcast(I32), 0)
         nc.vector.memset(moved_bytes[:].bitcast(I32), 0)
+        nc.vector.memset(w_plane[1][:].bitcast(I32), 0)
         make_identity(nc, ident[:])
 
         x_scale_words = x_scales.bitcast(I32)
         w_by_half = w_words.bitcast(I32).rearrange("e a p (h c) -> h p (e a) c", h=2)
-        w_scale_rows = w_scales.bitcast(I32).rearrange("e a (q r) c -> r q (e a) c", r=4)
+        w_scale_rows = w_scales.bitcast(I32).rearrange("e a (q r) (h c) -> h r q (e a) c", r=4, h=2)
 
         nc.sync.dma_start(offs_sb[:], offs)
         nc.scalar.dma_start(b_sb[:, :, 0:E], b.rearrange("(j p) e -> p j e", p=P))
@@ -72,7 +72,7 @@ def tile_moe_nxt_lin_bias_kernel(tc, x_words, x_scales, w_words, w_scales, b, wp
         nc.sync.dma_start(pos_sb[1][:], pos2)
         nc.sync.dma_start(w_sb[0][:].bitcast(I32), w_by_half[0])
         for r in range(4):
-            nc.scalar.dma_start(w_plane[r:P:32].bitcast(I32), w_scale_rows[r])
+            nc.scalar.dma_start(w_plane[0][r:P:32].bitcast(I32), w_scale_rows[0, r])
 
         for s0, s1 in spans(BYTE_CUTS):
             nc.vector.tensor_copy(slot_bytes[:, s0:s1], x_bytes[:].indirect(offs_sb[:, s0 // 16 : s1 // 16]))
@@ -81,7 +81,11 @@ def tile_moe_nxt_lin_bias_kernel(tc, x_words, x_scales, w_words, w_scales, b, wp
         slot_plane = [slot_bytes, moved_bytes]
         gate_sb = keep.tile([P, 2, T], F32, name="gate_sb")
         nc.sync.dma_start(gate_sb[:], gate[:, 0:P, :].rearrange("r p t -> p r t"))
-        nc.sync.dma_start(w_sb[1][:].bitcast(I32), w_by_half[1])
+        for r in range(4):
+            nc.sync.dma_start(w_plane[1][r:P:32].bitcast(I32), w_scale_rows[1, r])
+        for g in range(2):
+            rows = slice(g * E, (g + 1) * E)
+            nc.sync.dma_start(w_sb[1][:, rows, :].bitcast(I32), w_by_half[1, :, rows, :])
         wp_raw = keep.tile([P, 4, M], F32, name="wp_raw")
         nc.sync.dma_start(wp_raw[:], wp.rearrange("(p r) m -> p r m", r=4))
         for s0, s1 in spans(WORD_CUTS):
@@ -106,7 +110,7 @@ def tile_moe_nxt_lin_bias_kernel(tc, x_words, x_scales, w_words, w_scales, b, wp
                         nc.tensor.matmul_mx(
                             out=bank[:, (e - e0) * C : (e - e0 + 1) * C],
                             lhsT=w_sb[half][:, e * PASSES + a, word_bytes].bitcast(FP4X4),
-                            lhsT_scale=w_plane[:, e * PASSES + a, j * P : (j + 1) * P],
+                            lhsT_scale=w_plane[half][:, e * PASSES + a, P * (j % 2) : P * (j % 2 + 1)],
                             rhs=slot_words[a][:, slots].bitcast(FP8X4),
                             rhs_scale=slot_plane[a][:, slots],
                             start=(a == 0),
@@ -201,16 +205,16 @@ def tile_moe_nxt_lin_bias_kernel(tc, x_words, x_scales, w_words, w_scales, b, wp
         def parts_tile(name, width):
             return keep.tile([P, 2, width], F32, name=name, align_bytes=64)
 
-        experts(0, (0, 3, 6), (0, 1))
-        experts(1, (0, 3, 6), (3, 4))
-        experts(0, (6, 9), (2,))
+        experts(0, (0, 3, 6, 9), (0, 1, 2))
         experts(0, (9, 10), (6,), on_vector=True)
-        experts(1, (6, 10), (5,))
+        experts(1, (0, 4, 8, 10), (3, 4, 5))
         early_parts = [gated(0, 0, T, parts_tile("parts0", T))]
-        experts(2, (0, 4, 8, 10), (0, 1, 2))
+        experts(2, (0, 3, 5), (0, 1))
+        experts(3, (0, 3, 5), (3, 4))
         early_parts.append(gated(1, 0, T, parts_tile("parts1", T)))
-        experts(3, (0, 4, 8, 10), (3, 4, 5))
-        for j, banks in enumerate(((1, 2), (3, 4))):
+        experts(2, (5, 8, 10), (2, 6))
+        experts(3, (5, 7, 9, 10), (5, 7, 0))
+        for j, banks in enumerate(((2, 6), (5, 7))):
             for (t0, t1), number in zip(spans(BANK_CUTS), banks):
                 add_turned(j, t0, t1, early_parts[j], 0, number)
             if j == 0:
@@ -225,9 +229,9 @@ def tile_moe_nxt_lin_bias_kernel(tc, x_words, x_scales, w_words, w_scales, b, wp
                 parts = parts_tile("parts2", t1 - t0)
             else:
                 parts = late.tile([P, 2, t1 - t0], F32, name="parts2_%d" % i, offset=2048 * (i - 1))
-            add_turned(2, t0, t1, gated(2, t0, t1, parts), t0, (5, 6, 7)[i])
-            add_turned(3, t0, t1, gated(3, t0, t1, parts_tile("parts3_%d" % i, t1 - t0)), t0, 0)
-            grouped.append(turn_back(i, (7, 1, 2)[i], i == 1))
-        sums = [project(i, grouped[i], (7, 4, 3)[i]) for i in range(len(chunks))]
+            add_turned(2, t0, t1, gated(2, t0, t1, parts), t0, (0, 6, 3)[i])
+            add_turned(3, t0, t1, gated(3, t0, t1, parts_tile("parts3_%d" % i, t1 - t0)), t0, 1)
+            grouped.append(turn_back(i, (3, 4, 2)[i], i == 1))
+        sums = [project(i, grouped[i], (3, 5, 7)[i]) for i in range(len(chunks))]
         for i in range(len(chunks)):
             store(i, sums[i], i != 1)

@@ -8,6 +8,7 @@ S = E * C
 P = 128
 PASSES = K // 512
 NT = N // P
+BLOCKS = T // P
 
 FLOPS = 2 * S * K * N + 2 * T * N * M
 BYTES = K * T + K * T // 32 + E * K * N // 2 + E * K * N // 32 + 4 * (N * E + N * M + 2 * P * T + M * T) + 2 * P * (S + 2 * T) // 16
@@ -25,9 +26,10 @@ IDENTITY = mybir.ActivationFunctionType.Identity
 
 WORD_CUTS = (0, 384, 768, 1152, 1280)
 BYTE_CUTS = (0, 448, 896, 1280)
-TOKEN_CUTS = (0, 256, 512, 640)
+TOKEN_CUTS = (0, 256, 384, 512, 640)
 BANK_CUTS = (0, 512, 640)
 BANK_BYTES = 2048
+PARTS_BYTES = 2 * 2 * P * 4
 
 
 def spans(cuts):
@@ -50,44 +52,69 @@ def tile_moe_nxt_lin_bias_kernel(tc, x_words, x_scales, w_words, w_scales, b, wp
         slot_words = [keep.tile([P, S], U32, name="slot_words%d" % a, align_bytes=64) for a in range(PASSES)]
         slot_bytes = keep.tile([P, S], U8, name="slot_bytes", align_bytes=64)
         moved_bytes = keep.tile([P, S], U8, name="moved_bytes", align_bytes=64)
-        b_sb = late.tile([P, NT, 16], F32, name="b_sb", offset=2048 - 64)
+        b_sb = late.tile([P, NT, 16], F32, name="b_sb", offset=PARTS_BYTES - 128)
         ident = keep.tile([P, P], F32, name="ident")
 
-        nc.gpsimd.memset(x_bytes[:].bitcast(I32), 0)
+        gate_rows = keep.tile([P, P], F32, name="gate_rows")
+        zero = keep.tile([P, 1], F32, name="zero")
+        nc.vector.memset(zero[:], 0.0)
         nc.vector.memset(w_plane[0][:].bitcast(I32), 0)
         nc.vector.memset(moved_bytes[:].bitcast(I32), 0)
-        nc.vector.memset(w_plane[1][:].bitcast(I32), 0)
+        nc.gpsimd.memset(x_bytes[:].bitcast(I32), 0)
+        nc.gpsimd.memset(gate_rows[0 : P // 2, :], 0.0)
+        nc.gpsimd.dma_start(gate_rows[0 : 2 * BLOCKS, :], gate[:, 0, :].rearrange("r (k t) -> r k t", t=P))
         make_identity(nc, ident[:])
+        nc.gpsimd.memset(w_plane[1][:].bitcast(I32), 0)
 
         x_scale_words = x_scales.bitcast(I32)
         w_by_half = w_words.bitcast(I32).rearrange("e a p (h c) -> h p (e a) c", h=2)
         w_scale_rows = w_scales.bitcast(I32).rearrange("e a (q r) (h c) -> h r q (e a) c", r=4, h=2)
 
+        gate_sb = keep.tile([P, 2, T], F32, name="gate_sb")
+        wp_raw = keep.tile([P, 4, M], F32, name="wp_raw")
         nc.sync.dma_start(offs_sb[:], offs)
-        nc.scalar.dma_start(b_sb[:, :, 0:E], b.rearrange("(j p) e -> p j e", p=P))
+        nc.scalar.copy(gate_rows[P // 2 : P, :], zero[P // 2 : P, :].to_broadcast([P // 2, P]))
         for q in range(4):
             nc.sync.dma_start(x_bytes[32 * q : 32 * q + 8, :].bitcast(I32), x_scale_words[:, 4 * q : 4 * q + 4, :])
         nc.sync.dma_start(x_sb[:], x_words.rearrange("a p t r -> p a (t r)").bitcast(I32))
+
+        def load_scale_rows(half, rows):
+            for r in rows:
+                nc.sync.dma_start(w_plane[half][r:P:32].bitcast(I32), w_scale_rows[half, r])
+
+        load_scale_rows(0, range(0, 1))
+        nc.sync.dma_start(w_sb[0][:].bitcast(I32), w_by_half[0])
+        load_scale_rows(0, range(1, 4))
+        nc.sync.dma_start(b_sb[:, :, 0:E], b.rearrange("(j p) e -> p j e", p=P))
         nc.sync.dma_start(pos_sb[0][:], pos1)
         nc.sync.dma_start(pos_sb[1][:], pos2)
-        nc.sync.dma_start(w_sb[0][:].bitcast(I32), w_by_half[0])
-        for r in range(4):
-            nc.scalar.dma_start(w_plane[0][r:P:32].bitcast(I32), w_scale_rows[0, r])
+        nc.sync.dma_start(wp_raw[:], wp.rearrange("(p r) m -> p r m", r=4))
+        load_scale_rows(1, range(4))
+        for g in range(2):
+            rows = slice(g * E, (g + 1) * E)
+            nc.sync.dma_start(w_sb[1][:, rows, :].bitcast(I32), w_by_half[1, :, rows, :])
+
+        def bank_tile(shape, number):
+            return psum.tile(shape, F32, name="bank", offset=number * BANK_BYTES)
+
+        gate_cols = keep.tile([P, 2 * BLOCKS], F32, name="gate_cols")
+        bank = bank_tile([P, P], 4)
+        nc.tensor.transpose(bank[:], gate_rows[:], ident[:])
+        nc.scalar.copy(gate_cols[:], bank[:, 0 : 2 * BLOCKS])
+        gate_flat = gate_sb[:].rearrange("p r t -> p (r t)")
+        for (k0, k1), number in zip(spans((0, 4, 8, 2 * BLOCKS)), (5, 6, 7)):
+            bank = bank_tile([P, (k1 - k0) * P], number)
+            for k in range(k0, k1):
+                nc.tensor.transpose(
+                    bank[:, (k - k0) * P : (k - k0 + 1) * P], gate_cols[:, k : k + 1].to_broadcast([P, P]), ident[:]
+                )
+            nc.scalar.copy(gate_flat[:, k0 * P : k1 * P], bank[:])
 
         for s0, s1 in spans(BYTE_CUTS):
             nc.vector.tensor_copy(slot_bytes[:, s0:s1], x_bytes[:].indirect(offs_sb[:, s0 // 16 : s1 // 16]))
         for r in range(4):
-            nc.sync.dma_start(moved_bytes[r:P:32, :].bitcast(I32), slot_bytes[4 + r : P : 32, :].bitcast(I32))
+            nc.scalar.dma_start(moved_bytes[r:P:32, :].bitcast(I32), slot_bytes[4 + r : P : 32, :].bitcast(I32))
         slot_plane = [slot_bytes, moved_bytes]
-        gate_sb = keep.tile([P, 2, T], F32, name="gate_sb")
-        nc.sync.dma_start(gate_sb[:], gate[:, 0:P, :].rearrange("r p t -> p r t"))
-        for r in range(4):
-            nc.sync.dma_start(w_plane[1][r:P:32].bitcast(I32), w_scale_rows[1, r])
-        for g in range(2):
-            rows = slice(g * E, (g + 1) * E)
-            nc.sync.dma_start(w_sb[1][:, rows, :].bitcast(I32), w_by_half[1, :, rows, :])
-        wp_raw = keep.tile([P, 4, M], F32, name="wp_raw")
-        nc.sync.dma_start(wp_raw[:], wp.rearrange("(p r) m -> p r m", r=4))
         for s0, s1 in spans(WORD_CUTS):
             for a in range(PASSES):
                 nc.vector.tensor_copy(
@@ -96,10 +123,7 @@ def tile_moe_nxt_lin_bias_kernel(tc, x_words, x_scales, w_words, w_scales, b, wp
 
         y = [keep.tile([P, S], F32, name="y%d" % j) for j in range(NT)]
 
-        def bank_tile(shape, number):
-            return psum.tile(shape, F32, name="bank", offset=number * BANK_BYTES)
-
-        def experts(j, cuts, banks, on_vector=False):
+        def experts(j, cuts, banks):
             half, word_bytes = j // 2, slice(2 * P * (j % 2), 2 * P * (j % 2 + 1))
             for (e0, e1), number in zip(spans(cuts), banks):
                 bank = bank_tile([P, (e1 - e0) * C], number)
@@ -119,16 +143,13 @@ def tile_moe_nxt_lin_bias_kernel(tc, x_words, x_scales, w_words, w_scales, b, wp
                 for e in group:
                     slots = slice(e * C, (e + 1) * C)
                     sums = bank[:, (e - e0) * C : (e - e0 + 1) * C]
-                    if on_vector:
-                        nc.vector.tensor_scalar_add(y[j][:, slots], sums, b_sb[:, j, e : e + 1])
-                    else:
-                        nc.scalar.activation(y[j][:, slots], sums, IDENTITY, bias=b_sb[:, j, e : e + 1])
+                    nc.scalar.activation(y[j][:, slots], sums, IDENTITY, bias=b_sb[:, j, e : e + 1])
 
         wp_codes = keep.tile([P, M], U32, name="wp_codes", align_bytes=64)
         wp_plane = keep.tile([P, M], U8, name="wp_plane", align_bytes=64)
 
         chunks = spans(TOKEN_CUTS)
-        c_turned = keep.tile([P, T // P, 2, NT, 32, 2], BF16, name="c_turned", align_bytes=64)
+        c_turned = keep.tile([P, BLOCKS, 2, NT, 32, 2], BF16, name="c_turned", align_bytes=64)
 
         def gated(j, t0, t1, parts):
             for r in range(2):
@@ -156,19 +177,17 @@ def tile_moe_nxt_lin_bias_kernel(tc, x_words, x_scales, w_words, w_scales, b, wp
                 bank[:].rearrange("p (k q u d) -> p u k q d", q=32, u=2, d=2),
             )
 
-        def turn_back(i, number, on_vector):
+        def turn_back(i, number):
             t0, t1 = chunks[i]
             width = t1 - t0
             blocks = width // P
-            pairs = c_turned[:, t0 // P : t1 // P].rearrange("p k u j q d -> p (k u j q d)").bitcast(F32)
             bank = bank_tile([P, blocks, 2, P], number)
             for k in range(blocks):
+                pairs = c_turned[:, t0 // P + k].rearrange("p u j q d -> p (u j q d)").bitcast(F32)
                 for u in range(2):
-                    c0 = (2 * k + u) * P
-                    nc.tensor.transpose(bank[:, k, u, :], pairs[:, c0 : c0 + P], ident[:])
+                    nc.tensor.transpose(bank[:, k, u, :], pairs[:, u * P : (u + 1) * P], ident[:])
             grouped = keep.tile([P, width * 4], BF16, name="grouped%d" % i, align_bytes=64)
-            copy_out = nc.vector.tensor_copy if on_vector else nc.scalar.copy
-            copy_out(
+            nc.scalar.copy(
                 grouped[:].bitcast(F32).rearrange("p (k t u) -> p k t u", k=blocks, u=2),
                 bank[:].rearrange("p k u t -> p k t u"),
             )
@@ -193,45 +212,47 @@ def tile_moe_nxt_lin_bias_kernel(tc, x_words, x_scales, w_words, w_scales, b, wp
                 )
             return sums
 
-        def store(i, sums, on_vector):
+        def store(i, sums):
             t0, t1 = chunks[i]
             result = keep.tile([P, M // P, t1 - t0], F32, name="result%d" % i)
-            if on_vector:
-                nc.vector.tensor_copy(result[:], sums[:])
-            else:
-                nc.scalar.copy(result[:], sums[:])
+            nc.vector.tensor_copy(result[:], sums[:])
             nc.sync.dma_start(out.rearrange("(h p) t -> p h t", p=P)[:, :, t0:t1], result[:])
 
-        def parts_tile(name, width):
-            return keep.tile([P, 2, width], F32, name=name, align_bytes=64)
+        def parts_tile(tag, width):
+            return keep.tile([P, 2, width], F32, name="parts", tag=tag, align_bytes=64)
 
-        experts(0, (0, 3, 6, 9), (0, 1, 2))
-        experts(0, (9, 10), (6,), on_vector=True)
-        experts(1, (0, 4, 8, 10), (3, 4, 5))
-        early_parts = [gated(0, 0, T, parts_tile("parts0", T))]
-        experts(2, (0, 3, 5), (0, 1))
-        experts(3, (0, 3, 5), (3, 4))
-        early_parts.append(gated(1, 0, T, parts_tile("parts1", T)))
-        experts(2, (5, 8, 10), (2, 6))
-        experts(3, (5, 7, 9, 10), (5, 7, 0))
-        for j, banks in enumerate(((2, 6), (5, 7))):
+        wp_grouped = keep.tile([P, M, 4], BF16, name="wp_grouped", align_bytes=64)
+        nc.vector.tensor_copy(wp_grouped[:], wp_raw[:].rearrange("p r m -> p m r"))
+        nc.vector.quantize_mx(
+            out=wp_codes[:].bitcast(FP8X4), scales=wp_plane[:], in_=wp_grouped[:].rearrange("p m r -> p (m r)")
+        )
+        experts(0, (0, 3), (0,))
+        experts(1, (0, 3), (4,))
+        experts(0, (3, 6, 9, 10), (1, 2, 3))
+        experts(1, (3, 7, 10), (5, 6))
+        early_parts = [gated(j, 0, T, parts_tile("parts%d" % j, T)) for j in range(2)]
+        experts(2, (0, 3, 5), (7, 0))
+        experts(3, (0, 3, 5), (1, 2))
+        experts(2, (5, 8, 10), (3, 4))
+        experts(3, (5, 8, 10), (5, 6))
+        for j, banks in enumerate(((3, 4), (5, 6))):
             for (t0, t1), number in zip(spans(BANK_CUTS), banks):
                 add_turned(j, t0, t1, early_parts[j], 0, number)
-            if j == 0:
-                wp_grouped = keep.tile([P, M, 4], BF16, name="wp_grouped", tag="parts0", align_bytes=64)
-                nc.scalar.copy(wp_grouped[:], wp_raw[:].rearrange("p r m -> p m r"))
-                nc.vector.quantize_mx(
-                    out=wp_codes[:].bitcast(FP8X4), scales=wp_plane[:], in_=wp_grouped[:].rearrange("p m r -> p (m r)")
-                )
+        last = len(chunks) - 1
         grouped = []
         for i, (t0, t1) in enumerate(chunks):
-            if i == 0:
-                parts = parts_tile("parts2", t1 - t0)
+            if i == last:
+                first_sums = project(0, grouped[0], 3)
+            if i in (1, 2):
+                parts = late.tile([P, 2, 2, t1 - t0], F32, name="late_parts%d" % i, offset=(i - 1) * PARTS_BYTES)
             else:
-                parts = late.tile([P, 2, t1 - t0], F32, name="parts2_%d" % i, offset=2048 * (i - 1))
-            add_turned(2, t0, t1, gated(2, t0, t1, parts), t0, (0, 6, 3)[i])
-            add_turned(3, t0, t1, gated(3, t0, t1, parts_tile("parts3_%d" % i, t1 - t0)), t0, 1)
-            grouped.append(turn_back(i, (3, 4, 2)[i], i == 1))
-        sums = [project(i, grouped[i], (3, 5, 7)[i]) for i in range(len(chunks))]
-        for i in range(len(chunks)):
-            store(i, sums[i], i != 1)
+                tag = "grouped0" if i == last else "late_parts0"
+                parts = keep.tile([P, 2, 2, t1 - t0], F32, name="late_parts", tag=tag, align_bytes=64)
+            add_turned(2, t0, t1, gated(2, t0, t1, parts[:, 0]), t0, 1)
+            if i > 0:
+                grouped.append(turn_back(i - 1, (7, 0)[i % 2]))
+            add_turned(3, t0, t1, gated(3, t0, t1, parts[:, 1]), t0, 2)
+        grouped.append(turn_back(last, (7, 0)[(last + 1) % 2]))
+        store(0, first_sums)
+        for i in range(1, last + 1):
+            store(i, project(i, grouped[i], 3 + i))

@@ -47,7 +47,8 @@ def tile_moe_nxt_lin_bias_kernel(tc, x_words, x_scales, w_words, w_scales, b, wp
         pos_sb = [keep.tile([P, T // 16], U16, name="pos_sb%d" % r) for r in range(2)]
         x_bytes = keep.tile([P, T], U8, name="x_bytes", align_bytes=64)
         x_sb = keep.tile([P, PASSES, T], I32, name="x_sb", align_bytes=64)
-        w_sb = [keep.tile([P, E * PASSES, 4 * P], U8, name="w_sb%d" % h, align_bytes=256) for h in range(2)]
+        w_first = keep.tile([P, E, 8 * P], U8, name="w_first", align_bytes=256)
+        w_rest = [keep.tile([P, E, 4 * P], U8, name="w_rest%d" % h, align_bytes=256) for h in range(2)]
         w_plane = [keep.tile([P, E * PASSES, 2 * P], U8, name="w_plane%d" % h, align_bytes=256) for h in range(2)]
         slot_words = [keep.tile([P, S], U32, name="slot_words%d" % a, align_bytes=64) for a in range(PASSES)]
         slot_bytes = keep.tile([P, S], U8, name="slot_bytes", align_bytes=64)
@@ -57,25 +58,27 @@ def tile_moe_nxt_lin_bias_kernel(tc, x_words, x_scales, w_words, w_scales, b, wp
 
         gate_rows = keep.tile([P, P], F32, name="gate_rows")
         zero = keep.tile([P, 1], F32, name="zero")
-        nc.vector.memset(zero[:], 0.0)
         nc.vector.memset(w_plane[0][:].bitcast(I32), 0)
         nc.vector.memset(moved_bytes[:].bitcast(I32), 0)
         nc.gpsimd.memset(x_bytes[:].bitcast(I32), 0)
+        nc.gpsimd.memset(zero[:], 0.0)
         nc.gpsimd.memset(gate_rows[0 : P // 2, :], 0.0)
-        nc.gpsimd.dma_start(gate_rows[0 : 2 * BLOCKS, :], gate[:, 0, :].rearrange("r (k t) -> r k t", t=P))
         make_identity(nc, ident[:])
         nc.gpsimd.memset(w_plane[1][:].bitcast(I32), 0)
 
         x_scale_words = x_scales.bitcast(I32)
-        w_by_half = w_words.bitcast(I32).rearrange("e a p (h c) -> h p (e a) c", h=2)
+        w_rows = w_words.bitcast(I32).rearrange("e a p c -> p (e a) c")
         w_scale_rows = w_scales.bitcast(I32).rearrange("e a (q r) (h c) -> h r q (e a) c", r=4, h=2)
 
         gate_sb = keep.tile([P, 2, T], F32, name="gate_sb")
         wp_raw = keep.tile([P, 4, M], F32, name="wp_raw")
         nc.sync.dma_start(offs_sb[:], offs)
-        nc.scalar.copy(gate_rows[P // 2 : P, :], zero[P // 2 : P, :].to_broadcast([P // 2, P]))
         for q in range(4):
-            nc.sync.dma_start(x_bytes[32 * q : 32 * q + 8, :].bitcast(I32), x_scale_words[:, 4 * q : 4 * q + 4, :])
+            queue = (nc.sync, nc.scalar)[q % 2]
+            queue.dma_start(x_bytes[32 * q : 32 * q + 8, :].bitcast(I32), x_scale_words[:, 4 * q : 4 * q + 4, :])
+        nc.scalar.dma_start(gate_rows[0 : 2 * BLOCKS, :], gate[:, 0, :].rearrange("r (k t) -> r k t", t=P))
+        nc.scalar.dma_start(b_sb[:, :, 0:E], b.rearrange("(j p) e -> p j e", p=P))
+        nc.scalar.copy(gate_rows[P // 2 : P, :], zero[P // 2 : P, :].to_broadcast([P // 2, P]))
         nc.sync.dma_start(x_sb[:], x_words.rearrange("a p t r -> p a (t r)").bitcast(I32))
 
         def load_scale_rows(half, rows):
@@ -83,16 +86,14 @@ def tile_moe_nxt_lin_bias_kernel(tc, x_words, x_scales, w_words, w_scales, b, wp
                 nc.sync.dma_start(w_plane[half][r:P:32].bitcast(I32), w_scale_rows[half, r])
 
         load_scale_rows(0, range(0, 1))
-        nc.sync.dma_start(w_sb[0][:].bitcast(I32), w_by_half[0])
+        nc.sync.dma_start(w_first[:].bitcast(I32), w_rows[:, 0:E, :])
         load_scale_rows(0, range(1, 4))
-        nc.sync.dma_start(b_sb[:, :, 0:E], b.rearrange("(j p) e -> p j e", p=P))
+        nc.sync.dma_start(w_rest[0][:].bitcast(I32), w_rows[:, E : 2 * E, 0:P])
+        load_scale_rows(1, range(4))
         nc.sync.dma_start(pos_sb[0][:], pos1)
         nc.sync.dma_start(pos_sb[1][:], pos2)
+        nc.sync.dma_start(w_rest[1][:].bitcast(I32), w_rows[:, E : 2 * E, P : 2 * P])
         nc.sync.dma_start(wp_raw[:], wp.rearrange("(p r) m -> p r m", r=4))
-        load_scale_rows(1, range(4))
-        for g in range(2):
-            rows = slice(g * E, (g + 1) * E)
-            nc.sync.dma_start(w_sb[1][:, rows, :].bitcast(I32), w_by_half[1, :, rows, :])
 
         def bank_tile(shape, number):
             return psum.tile(shape, F32, name="bank", offset=number * BANK_BYTES)
@@ -123,8 +124,13 @@ def tile_moe_nxt_lin_bias_kernel(tc, x_words, x_scales, w_words, w_scales, b, wp
 
         y = [keep.tile([P, S], F32, name="y%d" % j) for j in range(NT)]
 
-        def experts(j, cuts, banks):
-            half, word_bytes = j // 2, slice(2 * P * (j % 2), 2 * P * (j % 2 + 1))
+        def weight_words(j, row):
+            if row < E:
+                return w_first[:, row, 2 * P * j : 2 * P * (j + 1)]
+            return w_rest[j // 2][:, row - E, 2 * P * (j % 2) : 2 * P * (j % 2 + 1)]
+
+        def experts(j, cuts, banks, on_vector=False):
+            half = j // 2
             for (e0, e1), number in zip(spans(cuts), banks):
                 bank = bank_tile([P, (e1 - e0) * C], number)
                 group = range(e0, e1)
@@ -133,7 +139,7 @@ def tile_moe_nxt_lin_bias_kernel(tc, x_words, x_scales, w_words, w_scales, b, wp
                     for a in range(PASSES):
                         nc.tensor.matmul_mx(
                             out=bank[:, (e - e0) * C : (e - e0 + 1) * C],
-                            lhsT=w_sb[half][:, e * PASSES + a, word_bytes].bitcast(FP4X4),
+                            lhsT=weight_words(j, e * PASSES + a).bitcast(FP4X4),
                             lhsT_scale=w_plane[half][:, e * PASSES + a, P * (j % 2) : P * (j % 2 + 1)],
                             rhs=slot_words[a][:, slots].bitcast(FP8X4),
                             rhs_scale=slot_plane[a][:, slots],
@@ -143,7 +149,10 @@ def tile_moe_nxt_lin_bias_kernel(tc, x_words, x_scales, w_words, w_scales, b, wp
                 for e in group:
                     slots = slice(e * C, (e + 1) * C)
                     sums = bank[:, (e - e0) * C : (e - e0 + 1) * C]
-                    nc.scalar.activation(y[j][:, slots], sums, IDENTITY, bias=b_sb[:, j, e : e + 1])
+                    if on_vector:
+                        nc.vector.tensor_scalar_add(y[j][:, slots], sums, b_sb[:, j, e : e + 1])
+                    else:
+                        nc.scalar.activation(y[j][:, slots], sums, IDENTITY, bias=b_sb[:, j, e : e + 1])
 
         wp_codes = keep.tile([P, M], U32, name="wp_codes", align_bytes=64)
         wp_plane = keep.tile([P, M], U8, name="wp_plane", align_bytes=64)
@@ -221,14 +230,10 @@ def tile_moe_nxt_lin_bias_kernel(tc, x_words, x_scales, w_words, w_scales, b, wp
         def parts_tile(tag, width):
             return keep.tile([P, 2, width], F32, name="parts", tag=tag, align_bytes=64)
 
-        wp_grouped = keep.tile([P, M, 4], BF16, name="wp_grouped", align_bytes=64)
-        nc.vector.tensor_copy(wp_grouped[:], wp_raw[:].rearrange("p r m -> p m r"))
-        nc.vector.quantize_mx(
-            out=wp_codes[:].bitcast(FP8X4), scales=wp_plane[:], in_=wp_grouped[:].rearrange("p m r -> p (m r)")
-        )
-        experts(0, (0, 3), (0,))
+        experts(0, (0, 3, 5), (0, 1))
         experts(1, (0, 3), (4,))
-        experts(0, (3, 6, 9, 10), (1, 2, 3))
+        experts(0, (5, 9), (2,))
+        experts(0, (9, 10), (3,), on_vector=True)
         experts(1, (3, 7, 10), (5, 6))
         early_parts = [gated(j, 0, T, parts_tile("parts%d" % j, T)) for j in range(2)]
         experts(2, (0, 3, 5), (7, 0))
@@ -238,6 +243,12 @@ def tile_moe_nxt_lin_bias_kernel(tc, x_words, x_scales, w_words, w_scales, b, wp
         for j, banks in enumerate(((3, 4), (5, 6))):
             for (t0, t1), number in zip(spans(BANK_CUTS), banks):
                 add_turned(j, t0, t1, early_parts[j], 0, number)
+            if j == 0:
+                wp_grouped = keep.tile([P, M, 4], BF16, name="wp_grouped", tag="parts0", align_bytes=64)
+                nc.scalar.copy(wp_grouped[:], wp_raw[:].rearrange("p r m -> p m r"))
+                nc.vector.quantize_mx(
+                    out=wp_codes[:].bitcast(FP8X4), scales=wp_plane[:], in_=wp_grouped[:].rearrange("p m r -> p (m r)")
+                )
         last = len(chunks) - 1
         grouped = []
         for i, (t0, t1) in enumerate(chunks):

@@ -29,7 +29,6 @@ BYTE_CUTS = (0, 448, 896, 1280)
 TOKEN_CUTS = (0, 256, 384, 512, 640)
 BANK_CUTS = (0, 512, 640)
 BANK_BYTES = 2048
-PARTS_BYTES = 2 * 2 * P * 4
 
 
 def spans(cuts):
@@ -40,20 +39,18 @@ def tile_moe_nxt_lin_bias_kernel(tc, x_words, x_scales, w_words, w_scales, b, wp
     nc = tc.nc
     with ExitStack() as ctx:
         keep = ctx.enter_context(tc.tile_pool(name="keep", bufs=1))
-        late = ctx.enter_context(tc.tile_pool(name="late", bufs=1))
         psum = ctx.enter_context(tc.psum_pool(name="psum", bufs=1))
 
         offs_sb = keep.tile([P, S // 16], U16, name="offs_sb")
         pos_sb = [keep.tile([P, T // 16], U16, name="pos_sb%d" % r) for r in range(2)]
         x_bytes = keep.tile([P, T], U8, name="x_bytes", align_bytes=64)
         x_sb = keep.tile([P, PASSES, T], I32, name="x_sb", align_bytes=64)
-        w_first = keep.tile([P, E, 8 * P], U8, name="w_first", align_bytes=256)
-        w_rest = [keep.tile([P, E, 4 * P], U8, name="w_rest%d" % h, align_bytes=256) for h in range(2)]
+        w_sb = [keep.tile([P, E * PASSES, 4 * P], U8, name="w_sb%d" % h, align_bytes=256) for h in range(2)]
         w_plane = [keep.tile([P, E * PASSES, 2 * P], U8, name="w_plane%d" % h, align_bytes=256) for h in range(2)]
         slot_words = [keep.tile([P, S], U32, name="slot_words%d" % a, align_bytes=64) for a in range(PASSES)]
         slot_bytes = keep.tile([P, S], U8, name="slot_bytes", align_bytes=64)
         moved_bytes = keep.tile([P, S], U8, name="moved_bytes", align_bytes=64)
-        b_sb = late.tile([P, NT, 16], F32, name="b_sb", offset=PARTS_BYTES - 128)
+        b_sb = keep.tile([P, NT, 16], F32, name="b_sb", align_bytes=64)
         ident = keep.tile([P, P], F32, name="ident")
 
         gate_rows = keep.tile([P, P], F32, name="gate_rows")
@@ -67,32 +64,40 @@ def tile_moe_nxt_lin_bias_kernel(tc, x_words, x_scales, w_words, w_scales, b, wp
         nc.gpsimd.memset(w_plane[1][:].bitcast(I32), 0)
 
         x_scale_words = x_scales.bitcast(I32)
-        w_rows = w_words.bitcast(I32).rearrange("e a p c -> p (e a) c")
+        w_by_half = w_words.bitcast(I32).rearrange("e a p (h c) -> h p (e a) c", h=2)
         w_scale_rows = w_scales.bitcast(I32).rearrange("e a (q r) (h c) -> h r q (e a) c", r=4, h=2)
 
         gate_sb = keep.tile([P, 2, T], F32, name="gate_sb")
         wp_raw = keep.tile([P, 4, M], F32, name="wp_raw")
-        nc.sync.dma_start(offs_sb[:], offs)
-        for q in range(4):
-            queue = (nc.sync, nc.scalar)[q % 2]
-            queue.dma_start(x_bytes[32 * q : 32 * q + 8, :].bitcast(I32), x_scale_words[:, 4 * q : 4 * q + 4, :])
-        nc.scalar.dma_start(gate_rows[0 : 2 * BLOCKS, :], gate[:, 0, :].rearrange("r (k t) -> r k t", t=P))
-        nc.scalar.dma_start(b_sb[:, :, 0:E], b.rearrange("(j p) e -> p j e", p=P))
-        nc.scalar.copy(gate_rows[P // 2 : P, :], zero[P // 2 : P, :].to_broadcast([P // 2, P]))
-        nc.sync.dma_start(x_sb[:], x_words.rearrange("a p t r -> p a (t r)").bitcast(I32))
 
-        def load_scale_rows(half, rows):
-            for r in rows:
+        def load_scale_rows(half):
+            for r in range(4):
                 nc.sync.dma_start(w_plane[half][r:P:32].bitcast(I32), w_scale_rows[half, r])
 
-        load_scale_rows(0, range(0, 1))
-        nc.sync.dma_start(w_first[:].bitcast(I32), w_rows[:, 0:E, :])
-        load_scale_rows(0, range(1, 4))
-        nc.sync.dma_start(w_rest[0][:].bitcast(I32), w_rows[:, E : 2 * E, 0:P])
-        load_scale_rows(1, range(4))
+        def load_weights(half, e0, e1):
+            rows = slice(e0 * PASSES, e1 * PASSES)
+            nc.sync.dma_start(w_sb[half][:, rows, :].bitcast(I32), w_by_half[half, :, rows, :])
+
+        nc.sync.dma_start(offs_sb[:], offs)
+        for q in range(4):
+            nc.sync.dma_start(x_bytes[32 * q : 32 * q + 8, :].bitcast(I32), x_scale_words[:, 4 * q : 4 * q + 4, :])
+        nc.scalar.dma_start(gate_rows[0 : 2 * BLOCKS, :], gate[:, 0, :].rearrange("r (k t) -> r k t", t=P))
+        nc.scalar.copy(gate_rows[P // 2 : P, :], zero[P // 2 : P, :].to_broadcast([P // 2, P]))
+        nc.sync.dma_start(x_sb[:], x_words.rearrange("a p t r -> p a (t r)").bitcast(I32))
+        nc.sync.dma_start(b_sb[:, :, 0:E], b.rearrange("(j p) e -> p j e", p=P))
+        load_scale_rows(0)
+        load_weights(0, 0, 3)
+        for s0, s1 in spans(BYTE_CUTS):
+            nc.vector.tensor_copy(slot_bytes[:, s0:s1], x_bytes[:].indirect(offs_sb[:, s0 // 16 : s1 // 16]))
+        for r in range(4):
+            nc.sync.dma_start(moved_bytes[r:P:32, :].bitcast(I32), slot_bytes[4 + r : P : 32, :].bitcast(I32))
+        slot_plane = [slot_bytes, moved_bytes]
+        load_weights(0, 3, E)
+        load_scale_rows(1)
         nc.sync.dma_start(pos_sb[0][:], pos1)
         nc.sync.dma_start(pos_sb[1][:], pos2)
-        nc.sync.dma_start(w_rest[1][:].bitcast(I32), w_rows[:, E : 2 * E, P : 2 * P])
+        load_weights(1, 0, 5)
+        load_weights(1, 5, E)
         nc.sync.dma_start(wp_raw[:], wp.rearrange("(p r) m -> p r m", r=4))
 
         def bank_tile(shape, number):
@@ -111,11 +116,6 @@ def tile_moe_nxt_lin_bias_kernel(tc, x_words, x_scales, w_words, w_scales, b, wp
                 )
             nc.scalar.copy(gate_flat[:, k0 * P : k1 * P], bank[:])
 
-        for s0, s1 in spans(BYTE_CUTS):
-            nc.vector.tensor_copy(slot_bytes[:, s0:s1], x_bytes[:].indirect(offs_sb[:, s0 // 16 : s1 // 16]))
-        for r in range(4):
-            nc.scalar.dma_start(moved_bytes[r:P:32, :].bitcast(I32), slot_bytes[4 + r : P : 32, :].bitcast(I32))
-        slot_plane = [slot_bytes, moved_bytes]
         for s0, s1 in spans(WORD_CUTS):
             for a in range(PASSES):
                 nc.vector.tensor_copy(
@@ -124,13 +124,8 @@ def tile_moe_nxt_lin_bias_kernel(tc, x_words, x_scales, w_words, w_scales, b, wp
 
         y = [keep.tile([P, S], F32, name="y%d" % j) for j in range(NT)]
 
-        def weight_words(j, row):
-            if row < E:
-                return w_first[:, row, 2 * P * j : 2 * P * (j + 1)]
-            return w_rest[j // 2][:, row - E, 2 * P * (j % 2) : 2 * P * (j % 2 + 1)]
-
         def experts(j, cuts, banks, on_vector=False):
-            half = j // 2
+            half, word_bytes = j // 2, slice(2 * P * (j % 2), 2 * P * (j % 2 + 1))
             for (e0, e1), number in zip(spans(cuts), banks):
                 bank = bank_tile([P, (e1 - e0) * C], number)
                 group = range(e0, e1)
@@ -139,7 +134,7 @@ def tile_moe_nxt_lin_bias_kernel(tc, x_words, x_scales, w_words, w_scales, b, wp
                     for a in range(PASSES):
                         nc.tensor.matmul_mx(
                             out=bank[:, (e - e0) * C : (e - e0 + 1) * C],
-                            lhsT=weight_words(j, e * PASSES + a).bitcast(FP4X4),
+                            lhsT=w_sb[half][:, e * PASSES + a, word_bytes].bitcast(FP4X4),
                             lhsT_scale=w_plane[half][:, e * PASSES + a, P * (j % 2) : P * (j % 2 + 1)],
                             rhs=slot_words[a][:, slots].bitcast(FP8X4),
                             rhs_scale=slot_plane[a][:, slots],
@@ -230,9 +225,9 @@ def tile_moe_nxt_lin_bias_kernel(tc, x_words, x_scales, w_words, w_scales, b, wp
         def parts_tile(tag, width):
             return keep.tile([P, 2, width], F32, name="parts", tag=tag, align_bytes=64)
 
-        experts(0, (0, 3, 5), (0, 1))
+        experts(0, (0, 3), (0,))
         experts(1, (0, 3), (4,))
-        experts(0, (5, 9), (2,))
+        experts(0, (3, 6, 9), (1, 2))
         experts(0, (9, 10), (3,), on_vector=True)
         experts(1, (3, 7, 10), (5, 6))
         early_parts = [gated(j, 0, T, parts_tile("parts%d" % j, T)) for j in range(2)]
@@ -250,20 +245,15 @@ def tile_moe_nxt_lin_bias_kernel(tc, x_words, x_scales, w_words, w_scales, b, wp
                     out=wp_codes[:].bitcast(FP8X4), scales=wp_plane[:], in_=wp_grouped[:].rearrange("p m r -> p (m r)")
                 )
         last = len(chunks) - 1
+        first_parts = keep.tile([P, 2, 2, TOKEN_CUTS[1]], F32, name="first_parts", align_bytes=64)
+        later_parts = keep.tile([P, last, 2, 2, P], F32, name="later_parts", tag="b_sb", align_bytes=64)
         grouped = []
         for i, (t0, t1) in enumerate(chunks):
-            if i == last:
-                first_sums = project(0, grouped[0], 3)
-            if i in (1, 2):
-                parts = late.tile([P, 2, 2, t1 - t0], F32, name="late_parts%d" % i, offset=(i - 1) * PARTS_BYTES)
-            else:
-                tag = "grouped0" if i == last else "late_parts0"
-                parts = keep.tile([P, 2, 2, t1 - t0], F32, name="late_parts", tag=tag, align_bytes=64)
+            parts = later_parts[:, i - 1] if i > 0 else first_parts[:]
             add_turned(2, t0, t1, gated(2, t0, t1, parts[:, 0]), t0, 1)
             if i > 0:
                 grouped.append(turn_back(i - 1, (7, 0)[i % 2]))
             add_turned(3, t0, t1, gated(3, t0, t1, parts[:, 1]), t0, 2)
         grouped.append(turn_back(last, (7, 0)[(last + 1) % 2]))
-        store(0, first_sums)
-        for i in range(1, last + 1):
-            store(i, project(i, grouped[i], 3 + i))
+        for i in range(last + 1):
+            store(i, project(i, grouped[i], (1, 2, 1, 3)[i]))

@@ -22,12 +22,13 @@ U8 = mybir.dt.uint8
 FP8X4 = mybir.dt.float8_e4m3fn_x4
 FP4X4 = mybir.dt.float4_e2m1fn_x4
 MULT = mybir.AluOpType.mult
+ADD = mybir.AluOpType.add
 IDENTITY = mybir.ActivationFunctionType.Identity
+COPY = mybir.ActivationFunctionType.Copy
 
 WORD_CUTS = (0, 384, 768, 1152, 1280)
 BYTE_CUTS = (0, 448, 896, 1280)
-TOKEN_CUTS = (0, 256, 384, 512, 640)
-BANK_CUTS = (0, 512, 640)
+TOKEN_CUTS = (128, 384, 512, 640)
 BANK_BYTES = 2048
 
 
@@ -86,6 +87,7 @@ def tile_moe_nxt_lin_bias_kernel(tc, x_words, x_scales, w_words, w_scales, b, wp
         nc.sync.dma_start(x_sb[:], x_words.rearrange("a p t r -> p a (t r)").bitcast(I32))
         nc.sync.dma_start(b_sb[:, :, 0:E], b.rearrange("(j p) e -> p j e", p=P))
         load_scale_rows(0)
+        nc.sync.dma_start(wp_raw[:], wp.rearrange("(p r) m -> p r m", r=4))
         load_weights(0, 0, 3)
         for s0, s1 in spans(BYTE_CUTS):
             nc.vector.tensor_copy(slot_bytes[:, s0:s1], x_bytes[:].indirect(offs_sb[:, s0 // 16 : s1 // 16]))
@@ -98,7 +100,6 @@ def tile_moe_nxt_lin_bias_kernel(tc, x_words, x_scales, w_words, w_scales, b, wp
         nc.sync.dma_start(pos_sb[1][:], pos2)
         load_weights(1, 0, 5)
         load_weights(1, 5, E)
-        nc.sync.dma_start(wp_raw[:], wp.rearrange("(p r) m -> p r m", r=4))
 
         def bank_tile(shape, number):
             return psum.tile(shape, F32, name="bank", offset=number * BANK_BYTES)
@@ -121,6 +122,14 @@ def tile_moe_nxt_lin_bias_kernel(tc, x_words, x_scales, w_words, w_scales, b, wp
                 nc.vector.tensor_copy(
                     slot_words[a][:, s0:s1], x_sb[:, a, :].bitcast(U32).indirect(offs_sb[:, s0 // 16 : s1 // 16])
                 )
+
+        wp_codes = keep.tile([P, M], U32, name="wp_codes", align_bytes=64)
+        wp_plane = keep.tile([P, M], U8, name="wp_plane", align_bytes=64)
+        wp_grouped = keep.tile([P, M, 4], BF16, name="wp_grouped", align_bytes=64)
+        nc.scalar.copy(wp_grouped[:], wp_raw[:].rearrange("p r m -> p m r"))
+        nc.vector.quantize_mx(
+            out=wp_codes[:].bitcast(FP8X4), scales=wp_plane[:], in_=wp_grouped[:].rearrange("p m r -> p (m r)")
+        )
 
         y = [keep.tile([P, S], F32, name="y%d" % j) for j in range(NT)]
 
@@ -148,9 +157,6 @@ def tile_moe_nxt_lin_bias_kernel(tc, x_words, x_scales, w_words, w_scales, b, wp
                         nc.vector.tensor_scalar_add(y[j][:, slots], sums, b_sb[:, j, e : e + 1])
                     else:
                         nc.scalar.activation(y[j][:, slots], sums, IDENTITY, bias=b_sb[:, j, e : e + 1])
-
-        wp_codes = keep.tile([P, M], U32, name="wp_codes", align_bytes=64)
-        wp_plane = keep.tile([P, M], U8, name="wp_plane", align_bytes=64)
 
         chunks = spans(TOKEN_CUTS)
         c_turned = keep.tile([P, BLOCKS, 2, NT, 32, 2], BF16, name="c_turned", align_bytes=64)
@@ -181,8 +187,34 @@ def tile_moe_nxt_lin_bias_kernel(tc, x_words, x_scales, w_words, w_scales, b, wp
                 bank[:].rearrange("p (k q u d) -> p u k q d", q=32, u=2, d=2),
             )
 
-        def turn_back(i, number):
-            t0, t1 = chunks[i]
+        def fetch_first(j, fetched):
+            for r in range(2):
+                nc.scalar.activation(fetched[:, r, j, :], y[j][:].indirect(pos_sb[r][:, 0 : P // 16]), COPY)
+
+        def gate_first(fetched, banks):
+            scaled = keep.tile([P, 2, N // 4, 2], F32, name="scaled", align_bytes=64)
+            turned = []
+            for r in range(2):
+                bank = bank_tile([P, N], banks[r])
+                for j in range(NT):
+                    nc.tensor.transpose(bank[:, j * P : (j + 1) * P], fetched[:, r, j, :], ident[:])
+                turned.append(bank[:].rearrange("t (q u d) -> t u q d", u=2, d=2))
+            nc.scalar.activation(scaled[:], turned[0], COPY, scale=gate_cols[:, 0:1])
+            return scaled, turned[1]
+
+        def add_first(scaled, turned):
+            for u in range(2):
+                nc.vector.scalar_tensor_tensor(
+                    c_turned[:, 0, u].rearrange("p j q d -> p (j q) d"),
+                    turned[:, u],
+                    gate_cols[:, BLOCKS : BLOCKS + 1],
+                    scaled[:, u],
+                    MULT,
+                    ADD,
+                )
+
+        def turn_back(t0, t1, number):
+            i = t0 // P
             width = t1 - t0
             blocks = width // P
             bank = bank_tile([P, blocks, 2, P], number)
@@ -197,8 +229,8 @@ def tile_moe_nxt_lin_bias_kernel(tc, x_words, x_scales, w_words, w_scales, b, wp
             )
             return grouped
 
-        def project(i, grouped, number):
-            t0, t1 = chunks[i]
+        def project(t0, t1, grouped, number):
+            i = t0 // P
             width = t1 - t0
             codes = keep.tile([P, width], U32, name="codes%d" % i, align_bytes=64)
             plane = keep.tile([P, width], U8, name="plane%d" % i, align_bytes=64)
@@ -216,10 +248,9 @@ def tile_moe_nxt_lin_bias_kernel(tc, x_words, x_scales, w_words, w_scales, b, wp
                 )
             return sums
 
-        def store(i, sums):
-            t0, t1 = chunks[i]
-            result = keep.tile([P, M // P, t1 - t0], F32, name="result%d" % i)
-            nc.vector.tensor_copy(result[:], sums[:])
+        def store(t0, t1, sums, copy):
+            result = keep.tile([P, M // P, t1 - t0], F32, name="result%d" % (t0 // P))
+            copy(result[:], sums[:])
             nc.sync.dma_start(out.rearrange("(h p) t -> p h t", p=P)[:, :, t0:t1], result[:])
 
         def parts_tile(tag, width):
@@ -230,30 +261,39 @@ def tile_moe_nxt_lin_bias_kernel(tc, x_words, x_scales, w_words, w_scales, b, wp
         experts(0, (3, 6, 9), (1, 2))
         experts(0, (9, 10), (3,), on_vector=True)
         experts(1, (3, 7, 10), (5, 6))
-        early_parts = [gated(j, 0, T, parts_tile("parts%d" % j, T)) for j in range(2)]
+        early_parts = [gated(j, P, T, parts_tile("parts%d" % j, T - P)) for j in range(2)]
+        fetched = keep.tile([P, 2, NT, P], F32, name="fetched", align_bytes=64)
         experts(2, (0, 3, 5), (7, 0))
         experts(3, (0, 3, 5), (1, 2))
+        fetch_first(0, fetched)
+        fetch_first(1, fetched)
         experts(2, (5, 8, 10), (3, 4))
         experts(3, (5, 8, 10), (5, 6))
-        for j, banks in enumerate(((3, 4), (5, 6))):
-            for (t0, t1), number in zip(spans(BANK_CUTS), banks):
-                add_turned(j, t0, t1, early_parts[j], 0, number)
-            if j == 0:
-                wp_grouped = keep.tile([P, M, 4], BF16, name="wp_grouped", tag="parts0", align_bytes=64)
-                nc.scalar.copy(wp_grouped[:], wp_raw[:].rearrange("p r m -> p m r"))
-                nc.vector.quantize_mx(
-                    out=wp_codes[:].bitcast(FP8X4), scales=wp_plane[:], in_=wp_grouped[:].rearrange("p m r -> p (m r)")
-                )
-        last = len(chunks) - 1
-        first_parts = keep.tile([P, 2, 2, TOKEN_CUTS[1]], F32, name="first_parts", align_bytes=64)
-        later_parts = keep.tile([P, last, 2, 2, P], F32, name="later_parts", tag="b_sb", align_bytes=64)
-        grouped = []
+        fetch_first(2, fetched)
+        fetch_first(3, fetched)
+        first_parts = keep.tile([P, 2, 2, TOKEN_CUTS[1] - TOKEN_CUTS[0]], F32, name="first_parts", align_bytes=64)
+        later_parts = keep.tile([P, 2, 2, 2, P], F32, name="later_parts", tag="b_sb", align_bytes=64)
+        parts = [first_parts[:], later_parts[:, 0], later_parts[:, 1]]
         for i, (t0, t1) in enumerate(chunks):
-            parts = later_parts[:, i - 1] if i > 0 else first_parts[:]
-            add_turned(2, t0, t1, gated(2, t0, t1, parts[:, 0]), t0, 1)
-            if i > 0:
-                grouped.append(turn_back(i - 1, (7, 0)[i % 2]))
-            add_turned(3, t0, t1, gated(3, t0, t1, parts[:, 1]), t0, 2)
-        grouped.append(turn_back(last, (7, 0)[(last + 1) % 2]))
-        for i in range(last + 1):
-            store(i, project(i, grouped[i], (1, 2, 1, 3)[i]))
+            for j in (2, 3):
+                gated(j, t0, t1, parts[i][:, j - 2])
+        wide, second, third = chunks
+        first = (0, P)
+        add_turned(0, P, T, early_parts[0], P, 3)
+        add_turned(1, P, T, early_parts[1], P, 4)
+        add_turned(2, *wide, parts[0][:, 0], wide[0], 1)
+        scaled, turned = gate_first(fetched, (7, 0))
+        add_turned(3, *wide, parts[0][:, 1], wide[0], 2)
+        add_first(scaled, turned)
+        grouped_wide = turn_back(*wide, 3)
+        add_turned(2, *second, parts[1][:, 0], second[0], 5)
+        add_turned(3, *second, parts[1][:, 1], second[0], 6)
+        add_turned(2, *third, parts[2][:, 0], third[0], 1)
+        add_turned(3, *third, parts[2][:, 1], third[0], 2)
+        grouped_second = turn_back(*second, 4)
+        grouped_first = turn_back(*first, 7)
+        grouped_third = turn_back(*third, 5)
+        store(*wide, project(*wide, grouped_wide, 6), nc.vector.tensor_copy)
+        store(*second, project(*second, grouped_second, 1), nc.scalar.copy)
+        store(*first, project(*first, grouped_first, 2), nc.scalar.copy)
+        store(*third, project(*third, grouped_third, 3), nc.vector.tensor_copy)

@@ -169,6 +169,9 @@ def tile_moe_nxt_lin_bias_kernel(tc, x_words, x_scales, w_words, w_scales, b, wp
             return parts
 
         def add_turned(j, t0, t1, parts, first, number):
+            round_turned(j, t0, t1, turn_and_add(t0, t1, parts, first, number))
+
+        def turn_and_add(t0, t1, parts, first, number):
             blocks = (t1 - t0) // P
             bank = bank_tile([P, blocks * P], number)
             for r in range(2):
@@ -182,6 +185,9 @@ def tile_moe_nxt_lin_bias_kernel(tc, x_words, x_scales, w_words, w_scales, b, wp
                         stop=(r == 1 and k == blocks - 1),
                         is_transpose=True,
                     )
+            return bank
+
+        def round_turned(j, t0, t1, bank):
             nc.scalar.copy(
                 c_turned[:, t0 // P : t1 // P, :, j].rearrange("p k u q d -> p u k q d"),
                 bank[:].rearrange("p (k q u d) -> p u k q d", q=32, u=2, d=2),
@@ -248,6 +254,17 @@ def tile_moe_nxt_lin_bias_kernel(tc, x_words, x_scales, w_words, w_scales, b, wp
                 )
             return sums
 
+        def warm_up(number):
+            nc.tensor.matmul_mx(
+                out=bank_tile([P, 512], number)[:],
+                lhsT=wp_codes[:, 0:P].bitcast(FP8X4),
+                lhsT_scale=wp_plane[:, 0:P],
+                rhs=slot_words[0][:, 0:512].bitcast(FP8X4),
+                rhs_scale=slot_bytes[:, 0:512],
+                start=True,
+                stop=True,
+            )
+
         def store(t0, t1, sums, copy):
             result = keep.tile([P, M // P, t1 - t0], F32, name="result%d" % (t0 // P))
             copy(result[:], sums[:])
@@ -268,8 +285,10 @@ def tile_moe_nxt_lin_bias_kernel(tc, x_words, x_scales, w_words, w_scales, b, wp
         fetch_first(0, fetched)
         fetch_first(1, fetched)
         experts(2, (5, 8, 10), (3, 4))
-        experts(3, (5, 8, 10), (5, 6))
+        experts(3, (5, 8, 10), (1, 2))
+        turned_early = turn_and_add(P, T, early_parts[0], P, 3)
         fetch_first(2, fetched)
+        round_turned(0, P, T, turned_early)
         fetch_first(3, fetched)
         first_parts = keep.tile([P, 2, 2, TOKEN_CUTS[1] - TOKEN_CUTS[0]], F32, name="first_parts", align_bytes=64)
         later_parts = keep.tile([P, 2, 2, 2, P], F32, name="later_parts", tag="b_sb", align_bytes=64)
@@ -279,15 +298,19 @@ def tile_moe_nxt_lin_bias_kernel(tc, x_words, x_scales, w_words, w_scales, b, wp
                 gated(j, t0, t1, parts[i][:, j - 2])
         wide, second, third = chunks
         first = (0, P)
-        add_turned(0, P, T, early_parts[0], P, 3)
         add_turned(1, P, T, early_parts[1], P, 4)
+        warm_up(2)
         add_turned(2, *wide, parts[0][:, 0], wide[0], 1)
         scaled, turned = gate_first(fetched, (7, 0))
+        warm_up(3)
         add_turned(3, *wide, parts[0][:, 1], wide[0], 2)
+        warm_up(4)
+        warm_up(7)
         add_first(scaled, turned)
         grouped_wide = turn_back(*wide, 3)
         add_turned(2, *second, parts[1][:, 0], second[0], 5)
         add_turned(3, *second, parts[1][:, 1], second[0], 6)
+        warm_up(2)
         add_turned(2, *third, parts[2][:, 0], third[0], 1)
         add_turned(3, *third, parts[2][:, 1], third[0], 2)
         grouped_second = turn_back(*second, 4)

@@ -168,8 +168,8 @@ def tile_moe_nxt_lin_bias_kernel(tc, x_words, x_scales, w_words, w_scales, b, wp
                 )
             return parts
 
-        def add_turned(j, t0, t1, parts, first, number):
-            round_turned(j, t0, t1, turn_and_add(t0, t1, parts, first, number))
+        def add_turned(j, t0, t1, parts, first, number, copy=nc.scalar.copy):
+            round_turned(j, t0, t1, turn_and_add(t0, t1, parts, first, number), copy)
 
         def turn_and_add(t0, t1, parts, first, number):
             blocks = (t1 - t0) // P
@@ -187,8 +187,8 @@ def tile_moe_nxt_lin_bias_kernel(tc, x_words, x_scales, w_words, w_scales, b, wp
                     )
             return bank
 
-        def round_turned(j, t0, t1, bank):
-            nc.scalar.copy(
+        def round_turned(j, t0, t1, bank, copy=nc.scalar.copy):
+            copy(
                 c_turned[:, t0 // P : t1 // P, :, j].rearrange("p k u q d -> p u k q d"),
                 bank[:].rearrange("p (k q u d) -> p u k q d", q=32, u=2, d=2),
             )
@@ -219,7 +219,7 @@ def tile_moe_nxt_lin_bias_kernel(tc, x_words, x_scales, w_words, w_scales, b, wp
                     ADD,
                 )
 
-        def turn_back(t0, t1, number):
+        def turn_back(t0, t1, number, copy=nc.scalar.copy):
             i = t0 // P
             width = t1 - t0
             blocks = width // P
@@ -229,19 +229,21 @@ def tile_moe_nxt_lin_bias_kernel(tc, x_words, x_scales, w_words, w_scales, b, wp
                 for u in range(2):
                     nc.tensor.transpose(bank[:, k, u, :], pairs[:, u * P : (u + 1) * P], ident[:])
             grouped = keep.tile([P, width * 4], BF16, name="grouped%d" % i, align_bytes=64)
-            nc.scalar.copy(
+            copy(
                 grouped[:].bitcast(F32).rearrange("p (k t u) -> p k t u", k=blocks, u=2),
                 bank[:].rearrange("p k u t -> p k t u"),
             )
             return grouped
 
-        def project(t0, t1, grouped, number):
-            i = t0 // P
-            width = t1 - t0
-            codes = keep.tile([P, width], U32, name="codes%d" % i, align_bytes=64)
-            plane = keep.tile([P, width], U8, name="plane%d" % i, align_bytes=64)
+        def quantise(t0, t1, grouped):
+            codes = keep.tile([P, t1 - t0], U32, name="codes%d" % (t0 // P), align_bytes=64)
+            plane = keep.tile([P, t1 - t0], U8, name="plane%d" % (t0 // P), align_bytes=64)
             nc.vector.quantize_mx(out=codes[:].bitcast(FP8X4), scales=plane[:], in_=grouped[:])
-            sums = bank_tile([P, M // P, width], number)
+            return codes, plane
+
+        def multiply(t0, t1, quantised, number):
+            codes, plane = quantised
+            sums = bank_tile([P, M // P, t1 - t0], number)
             for h in range(M // P):
                 nc.tensor.matmul_mx(
                     out=sums[:, h, :],
@@ -253,6 +255,26 @@ def tile_moe_nxt_lin_bias_kernel(tc, x_words, x_scales, w_words, w_scales, b, wp
                     stop=True,
                 )
             return sums
+
+        def project(t0, t1, grouped, number):
+            return multiply(t0, t1, quantise(t0, t1, grouped), number)
+
+        def store_halves(t0, t1, quantised, banks, copies):
+            codes, plane = quantised
+            for h in range(M // P):
+                sums = bank_tile([P, t1 - t0], banks[h])
+                nc.tensor.matmul_mx(
+                    out=sums[:],
+                    lhsT=wp_codes[:, h * P : (h + 1) * P].bitcast(FP8X4),
+                    lhsT_scale=wp_plane[:, h * P : (h + 1) * P],
+                    rhs=codes[:].bitcast(FP8X4),
+                    rhs_scale=plane[:],
+                    start=True,
+                    stop=True,
+                )
+                result = keep.tile([P, t1 - t0], F32, name="result%d_%d" % (t0 // P, h))
+                copies[h](result[:], sums[:])
+                nc.sync.dma_start(out[h * P : (h + 1) * P, t0:t1], result[:])
 
         def warm_up(number):
             nc.tensor.matmul_mx(
@@ -311,12 +333,12 @@ def tile_moe_nxt_lin_bias_kernel(tc, x_words, x_scales, w_words, w_scales, b, wp
         add_turned(2, *second, parts[1][:, 0], second[0], 5)
         add_turned(3, *second, parts[1][:, 1], second[0], 6)
         warm_up(2)
-        add_turned(2, *third, parts[2][:, 0], third[0], 1)
-        add_turned(3, *third, parts[2][:, 1], third[0], 2)
+        add_turned(2, *third, parts[2][:, 0], third[0], 1, nc.vector.tensor_copy)
+        add_turned(3, *third, parts[2][:, 1], third[0], 2, nc.vector.tensor_copy)
         grouped_second = turn_back(*second, 4)
         grouped_first = turn_back(*first, 7)
         grouped_third = turn_back(*third, 5)
-        store(*wide, project(*wide, grouped_wide, 6), nc.vector.tensor_copy)
+        store_halves(*wide, quantise(*wide, grouped_wide), (6, 0), (nc.vector.tensor_copy, nc.scalar.copy))
         store(*second, project(*second, grouped_second, 1), nc.scalar.copy)
         store(*first, project(*first, grouped_first, 2), nc.scalar.copy)
         store(*third, project(*third, grouped_third, 3), nc.vector.tensor_copy)

@@ -108,14 +108,12 @@ def tile_moe_nxt_lin_bias_kernel(tc, x_words, x_scales, w_words, w_scales, b, wp
         bank = bank_tile([P, P], 4)
         nc.tensor.transpose(bank[:], gate_rows[:], ident[:])
         nc.scalar.copy(gate_cols[:], bank[:, 0 : 2 * BLOCKS])
-        gate_flat = gate_sb[:].rearrange("p r t -> p (r t)")
-        for (k0, k1), number in zip(spans((0, 4, 8, 2 * BLOCKS)), (5, 6, 7)):
-            bank = bank_tile([P, (k1 - k0) * P], number)
-            for k in range(k0, k1):
-                nc.tensor.transpose(
-                    bank[:, (k - k0) * P : (k - k0 + 1) * P], gate_cols[:, k : k + 1].to_broadcast([P, P]), ident[:]
-                )
-            nc.scalar.copy(gate_flat[:, k0 * P : k1 * P], bank[:])
+        for r in range(2):
+            bank = bank_tile([P, T - P], 5 + r)
+            for k in range(1, BLOCKS):
+                column = gate_cols[:, r * BLOCKS + k : r * BLOCKS + k + 1]
+                nc.tensor.transpose(bank[:, (k - 1) * P : k * P], column.to_broadcast([P, P]), ident[:])
+            nc.scalar.copy(gate_sb[:, r, P:T], bank[:])
 
         for s0, s1 in spans(WORD_CUTS):
             for a in range(PASSES):
@@ -321,10 +319,8 @@ def tile_moe_nxt_lin_bias_kernel(tc, x_words, x_scales, w_words, w_scales, b, wp
         wide, second, third = chunks
         first = (0, P)
         add_turned(1, P, T, early_parts[1], P, 4)
-        warm_up(2)
         add_turned(2, *wide, parts[0][:, 0], wide[0], 1)
         scaled, turned = gate_first(fetched, (7, 0))
-        warm_up(3)
         add_turned(3, *wide, parts[0][:, 1], wide[0], 2)
         warm_up(4)
         warm_up(7)
@@ -332,7 +328,6 @@ def tile_moe_nxt_lin_bias_kernel(tc, x_words, x_scales, w_words, w_scales, b, wp
         grouped_wide = turn_back(*wide, 3)
         add_turned(2, *second, parts[1][:, 0], second[0], 5)
         add_turned(3, *second, parts[1][:, 1], second[0], 6)
-        warm_up(2)
         add_turned(2, *third, parts[2][:, 0], third[0], 1, nc.vector.tensor_copy)
         add_turned(3, *third, parts[2][:, 1], third[0], 2, nc.vector.tensor_copy)
         grouped_second = turn_back(*second, 4)

@@ -257,22 +257,21 @@ def tile_moe_nxt_lin_bias_kernel(tc, x_words, x_scales, w_words, w_scales, b, wp
         def project(t0, t1, grouped, number):
             return multiply(t0, t1, quantise(t0, t1, grouped), number)
 
-        def store_halves(t0, t1, quantised, banks, copies):
+        def store_half(t0, t1, h, quantised, number, copy, tag):
             codes, plane = quantised
-            for h in range(M // P):
-                sums = bank_tile([P, t1 - t0], banks[h])
-                nc.tensor.matmul_mx(
-                    out=sums[:],
-                    lhsT=wp_codes[:, h * P : (h + 1) * P].bitcast(FP8X4),
-                    lhsT_scale=wp_plane[:, h * P : (h + 1) * P],
-                    rhs=codes[:].bitcast(FP8X4),
-                    rhs_scale=plane[:],
-                    start=True,
-                    stop=True,
-                )
-                result = keep.tile([P, t1 - t0], F32, name="result%d_%d" % (t0 // P, h))
-                copies[h](result[:], sums[:])
-                nc.sync.dma_start(out[h * P : (h + 1) * P, t0:t1], result[:])
+            sums = bank_tile([P, t1 - t0], number)
+            nc.tensor.matmul_mx(
+                out=sums[:],
+                lhsT=wp_codes[:, h * P : (h + 1) * P].bitcast(FP8X4),
+                lhsT_scale=wp_plane[:, h * P : (h + 1) * P],
+                rhs=codes[:].bitcast(FP8X4),
+                rhs_scale=plane[:],
+                start=True,
+                stop=True,
+            )
+            result = keep.tile([P, t1 - t0], F32, name="result", tag=tag, align_bytes=64)
+            copy(result[:], sums[:])
+            nc.sync.dma_start(out[h * P : (h + 1) * P, t0:t1], result[:])
 
         def warm_up(number):
             nc.tensor.matmul_mx(
@@ -325,15 +324,18 @@ def tile_moe_nxt_lin_bias_kernel(tc, x_words, x_scales, w_words, w_scales, b, wp
         warm_up(4)
         warm_up(7)
         add_first(scaled, turned)
-        grouped_wide = turn_back(*wide, 3)
         add_turned(2, *second, parts[1][:, 0], second[0], 5)
         add_turned(3, *second, parts[1][:, 1], second[0], 6)
+        grouped_wide = turn_back(*wide, 3)
         add_turned(2, *third, parts[2][:, 0], third[0], 1, nc.vector.tensor_copy)
         add_turned(3, *third, parts[2][:, 1], third[0], 2, nc.vector.tensor_copy)
         grouped_second = turn_back(*second, 4)
         grouped_first = turn_back(*first, 7)
         grouped_third = turn_back(*third, 5)
-        store_halves(*wide, quantise(*wide, grouped_wide), (6, 0), (nc.vector.tensor_copy, nc.scalar.copy))
-        store(*second, project(*second, grouped_second, 1), nc.scalar.copy)
-        store(*first, project(*first, grouped_first, 2), nc.scalar.copy)
-        store(*third, project(*third, grouped_third, 3), nc.vector.tensor_copy)
+        order = ((wide, grouped_wide), (second, grouped_second), (first, grouped_first), (third, grouped_third))
+        quantised = [quantise(*chunk, grouped) for chunk, grouped in order]
+        store_half(*wide, 0, quantised[0], 6, nc.scalar.copy, "result")
+        store(*second, multiply(*second, quantised[1], 1), nc.scalar.copy)
+        store_half(*wide, 1, quantised[0], 0, nc.vector.tensor_copy, "grouped%d" % (third[0] // P))
+        store(*first, multiply(*first, quantised[2], 2), nc.scalar.copy)
+        store(*third, multiply(*third, quantised[3], 3), nc.vector.tensor_copy)

from contextlib import ExitStack

import concourse.mybir as mybir
from concourse.masks import make_identity

K, T, E, C, N, M = 1024, 640, 10, 128, 512, 256
S = E * C
P = 128
PASSES = K // 512
NT = N // P
BLOCKS = T // P

FLOPS = 2 * S * K * N + 2 * T * N * M
BYTES = K * T + K * T // 32 + E * K * N // 2 + E * K * N // 32 + 4 * (N * E + N * M + 2 * P * T + M * T) + 2 * P * (S + 2 * T) // 16

F32 = mybir.dt.float32
BF16 = mybir.dt.bfloat16
I32 = mybir.dt.int32
U32 = mybir.dt.uint32
U16 = mybir.dt.uint16
U8 = mybir.dt.uint8
FP8X4 = mybir.dt.float8_e4m3fn_x4
FP4X4 = mybir.dt.float4_e2m1fn_x4
MULT = mybir.AluOpType.mult
ADD = mybir.AluOpType.add
IDENTITY = mybir.ActivationFunctionType.Identity
COPY = mybir.ActivationFunctionType.Copy

WORD_CUTS = (0, 384, 768, 1152, 1280)
BYTE_CUTS = (0, 448, 896, 1280)
TOKEN_CUTS = (128, 384, 512, 640)
BANK_BYTES = 2048


def spans(cuts):
    return list(zip(cuts[:-1], cuts[1:]))


def tile_moe_nxt_lin_bias_kernel(tc, x_words, x_scales, w_words, w_scales, b, wp, gate, offs, pos1, pos2, out):
    nc = tc.nc
    with ExitStack() as ctx:
        keep = ctx.enter_context(tc.tile_pool(name="keep", bufs=1))
        psum = ctx.enter_context(tc.psum_pool(name="psum", bufs=1))

        offs_sb = keep.tile([P, S // 16], U16, name="offs_sb")
        pos_sb = [keep.tile([P, T // 16], U16, name="pos_sb%d" % r) for r in range(2)]
        x_bytes = keep.tile([P, T], U8, name="x_bytes", align_bytes=64)
        x_sb = keep.tile([P, PASSES, T], I32, name="x_sb", align_bytes=64)
        w_sb = [keep.tile([P, E * PASSES, 4 * P], U8, name="w_sb%d" % h, align_bytes=256) for h in range(2)]
        w_plane = [keep.tile([P, E * PASSES, 2 * P], U8, name="w_plane%d" % h, align_bytes=256) for h in range(2)]
        slot_words = [keep.tile([P, S], U32, name="slot_words%d" % a, align_bytes=64) for a in range(PASSES)]
        slot_bytes = keep.tile([P, S], U8, name="slot_bytes", align_bytes=64)
        moved_bytes = keep.tile([P, S], U8, name="moved_bytes", align_bytes=64)
        b_sb = keep.tile([P, NT, 16], F32, name="b_sb", align_bytes=64)
        ident = keep.tile([P, P], F32, name="ident")

        gate_rows = keep.tile([P, P], F32, name="gate_rows")
        zero = keep.tile([P, 1], F32, name="zero")
        nc.vector.memset(w_plane[0][:].bitcast(I32), 0)
        nc.vector.memset(moved_bytes[:].bitcast(I32), 0)
        nc.gpsimd.memset(x_bytes[:].bitcast(I32), 0)
        nc.gpsimd.memset(zero[:], 0.0)
        nc.gpsimd.memset(gate_rows[0 : P // 2, :], 0.0)
        make_identity(nc, ident[:])
        nc.gpsimd.memset(w_plane[1][:].bitcast(I32), 0)

        x_scale_words = x_scales.bitcast(I32)
        w_by_half = w_words.bitcast(I32).rearrange("e a p (h c) -> h p (e a) c", h=2)
        w_scale_rows = w_scales.bitcast(I32).rearrange("e a (q r) (h c) -> h r q (e a) c", r=4, h=2)

        gate_sb = keep.tile([P, 2, T], F32, name="gate_sb")
        wp_raw = keep.tile([P, 4, M], F32, name="wp_raw")

        def load_scale_rows(half):
            for r in range(4):
                nc.sync.dma_start(w_plane[half][r:P:32].bitcast(I32), w_scale_rows[half, r])

        def load_weights(half, e0, e1):
            rows = slice(e0 * PASSES, e1 * PASSES)
            nc.sync.dma_start(w_sb[half][:, rows, :].bitcast(I32), w_by_half[half, :, rows, :])

        nc.sync.dma_start(offs_sb[:], offs)
        for q in range(4):
            nc.sync.dma_start(x_bytes[32 * q : 32 * q + 8, :].bitcast(I32), x_scale_words[:, 4 * q : 4 * q + 4, :])
        nc.scalar.dma_start(gate_rows[0 : 2 * BLOCKS, :], gate[:, 0, :].rearrange("r (k t) -> r k t", t=P))
        nc.scalar.copy(gate_rows[P // 2 : P, :], zero[P // 2 : P, :].to_broadcast([P // 2, P]))
        nc.sync.dma_start(x_sb[:], x_words.rearrange("a p t r -> p a (t r)").bitcast(I32))
        nc.sync.dma_start(b_sb[:, :, 0:E], b.rearrange("(j p) e -> p j e", p=P))
        load_scale_rows(0)
        nc.sync.dma_start(wp_raw[:], wp.rearrange("(p r) m -> p r m", r=4))
        load_weights(0, 0, 3)
        for s0, s1 in spans(BYTE_CUTS):
            nc.vector.tensor_copy(slot_bytes[:, s0:s1], x_bytes[:].indirect(offs_sb[:, s0 // 16 : s1 // 16]))
        for r in range(4):
            nc.sync.dma_start(moved_bytes[r:P:32, :].bitcast(I32), slot_bytes[4 + r : P : 32, :].bitcast(I32))
        slot_plane = [slot_bytes, moved_bytes]
        load_weights(0, 3, E)
        load_scale_rows(1)
        nc.sync.dma_start(pos_sb[0][:], pos1)
        nc.sync.dma_start(pos_sb[1][:], pos2)
        load_weights(1, 0, 5)
        load_weights(1, 5, E)

        def bank_tile(shape, number):
            return psum.tile(shape, F32, name="bank", offset=number * BANK_BYTES)

        gate_cols = keep.tile([P, 2 * BLOCKS], F32, name="gate_cols")
        bank = bank_tile([P, P], 4)
        nc.tensor.transpose(bank[:], gate_rows[:], ident[:])
        nc.scalar.copy(gate_cols[:], bank[:, 0 : 2 * BLOCKS])
        for r in range(2):
            bank = bank_tile([P, T - P], 5 + r)
            for k in range(1, BLOCKS):
                column = gate_cols[:, r * BLOCKS + k : r * BLOCKS + k + 1]
                nc.tensor.transpose(bank[:, (k - 1) * P : k * P], column.to_broadcast([P, P]), ident[:])
            nc.scalar.copy(gate_sb[:, r, P:T], bank[:])

        for s0, s1 in spans(WORD_CUTS):
            for a in range(PASSES):
                nc.vector.tensor_copy(
                    slot_words[a][:, s0:s1], x_sb[:, a, :].bitcast(U32).indirect(offs_sb[:, s0 // 16 : s1 // 16])
                )

        wp_codes = keep.tile([P, M], U32, name="wp_codes", align_bytes=64)
        wp_plane = keep.tile([P, M], U8, name="wp_plane", align_bytes=64)
        wp_grouped = keep.tile([P, M, 4], BF16, name="wp_grouped", align_bytes=64)
        nc.scalar.copy(wp_grouped[:], wp_raw[:].rearrange("p r m -> p m r"))
        nc.vector.quantize_mx(
            out=wp_codes[:].bitcast(FP8X4), scales=wp_plane[:], in_=wp_grouped[:].rearrange("p m r -> p (m r)")
        )

        y = [keep.tile([P, S], F32, name="y%d" % j) for j in range(NT)]

        def experts(j, cuts, banks, on_vector=False):
            half, word_bytes = j // 2, slice(2 * P * (j % 2), 2 * P * (j % 2 + 1))
            for (e0, e1), number in zip(spans(cuts), banks):
                bank = bank_tile([P, (e1 - e0) * C], number)
                group = range(e0, e1)
                for e in group:
                    slots = slice(e * C, (e + 1) * C)
                    for a in range(PASSES):
                        nc.tensor.matmul_mx(
                            out=bank[:, (e - e0) * C : (e - e0 + 1) * C],
                            lhsT=w_sb[half][:, e * PASSES + a, word_bytes].bitcast(FP4X4),
                            lhsT_scale=w_plane[half][:, e * PASSES + a, P * (j % 2) : P * (j % 2 + 1)],
                            rhs=slot_words[a][:, slots].bitcast(FP8X4),
                            rhs_scale=slot_plane[a][:, slots],
                            start=(a == 0),
                            stop=(a == PASSES - 1),
                        )
                for e in group:
                    slots = slice(e * C, (e + 1) * C)
                    sums = bank[:, (e - e0) * C : (e - e0 + 1) * C]
                    if on_vector:
                        nc.vector.tensor_scalar_add(y[j][:, slots], sums, b_sb[:, j, e : e + 1])
                    else:
                        nc.scalar.activation(y[j][:, slots], sums, IDENTITY, bias=b_sb[:, j, e : e + 1])

        chunks = spans(TOKEN_CUTS)
        c_turned = keep.tile([P, BLOCKS, 2, NT, 32, 2], BF16, name="c_turned", align_bytes=64)

        def gated(j, t0, t1, parts):
            for r in range(2):
                nc.vector.tensor_tensor(
                    parts[:, r, :], y[j][:].indirect(pos_sb[r][:, t0 // 16 : t1 // 16]), gate_sb[:, r, t0:t1], MULT
                )
            return parts

        def add_turned(j, t0, t1, parts, first, number, copy=nc.scalar.copy):
            round_turned(j, t0, t1, turn_and_add(t0, t1, parts, first, number), copy)

        def turn_and_add(t0, t1, parts, first, number):
            blocks = (t1 - t0) // P
            bank = bank_tile([P, blocks * P], number)
            for r in range(2):
                for k in range(blocks):
                    c0 = t0 - first + k * P
                    nc.tensor.matmul(
                        bank[:, k * P : (k + 1) * P],
                        lhsT=parts[:, r, c0 : c0 + P],
                        rhs=ident[:],
                        start=(r == 0 and k == 0),
                        stop=(r == 1 and k == blocks - 1),
                        is_transpose=True,
                    )
            return bank

        def round_turned(j, t0, t1, bank, copy=nc.scalar.copy):
            copy(
                c_turned[:, t0 // P : t1 // P, :, j].rearrange("p k u q d -> p u k q d"),
                bank[:].rearrange("p (k q u d) -> p u k q d", q=32, u=2, d=2),
            )

        def fetch_first(j, fetched):
            for r in range(2):
                nc.scalar.activation(fetched[:, r, j, :], y[j][:].indirect(pos_sb[r][:, 0 : P // 16]), COPY)

        def gate_first(fetched, banks):
            scaled = keep.tile([P, 2, N // 4, 2], F32, name="scaled", align_bytes=64)
            turned = []
            for r in range(2):
                bank = bank_tile([P, N], banks[r])
                for j in range(NT):
                    nc.tensor.transpose(bank[:, j * P : (j + 1) * P], fetched[:, r, j, :], ident[:])
                turned.append(bank[:].rearrange("t (q u d) -> t u q d", u=2, d=2))
            nc.scalar.activation(scaled[:], turned[0], COPY, scale=gate_cols[:, 0:1])
            return scaled, turned[1]

        def add_first(scaled, turned):
            for u in range(2):
                nc.vector.scalar_tensor_tensor(
                    c_turned[:, 0, u].rearrange("p j q d -> p (j q) d"),
                    turned[:, u],
                    gate_cols[:, BLOCKS : BLOCKS + 1],
                    scaled[:, u],
                    MULT,
                    ADD,
                )

        def turn_back(t0, t1, number, copy=nc.scalar.copy):
            i = t0 // P
            width = t1 - t0
            blocks = width // P
            bank = bank_tile([P, blocks, 2, P], number)
            for k in range(blocks):
                pairs = c_turned[:, t0 // P + k].rearrange("p u j q d -> p (u j q d)").bitcast(F32)
                for u in range(2):
                    nc.tensor.transpose(bank[:, k, u, :], pairs[:, u * P : (u + 1) * P], ident[:])
            grouped = keep.tile([P, width * 4], BF16, name="grouped%d" % i, align_bytes=64)
            copy(
                grouped[:].bitcast(F32).rearrange("p (k t u) -> p k t u", k=blocks, u=2),
                bank[:].rearrange("p k u t -> p k t u"),
            )
            return grouped

        def quantise(t0, t1, grouped):
            codes = keep.tile([P, t1 - t0], U32, name="codes%d" % (t0 // P), align_bytes=64)
            plane = keep.tile([P, t1 - t0], U8, name="plane%d" % (t0 // P), align_bytes=64)
            nc.vector.quantize_mx(out=codes[:].bitcast(FP8X4), scales=plane[:], in_=grouped[:])
            return codes, plane

        def multiply(t0, t1, quantised, number):
            codes, plane = quantised
            sums = bank_tile([P, M // P, t1 - t0], number)
            for h in range(M // P):
                nc.tensor.matmul_mx(
                    out=sums[:, h, :],
                    lhsT=wp_codes[:, h * P : (h + 1) * P].bitcast(FP8X4),
                    lhsT_scale=wp_plane[:, h * P : (h + 1) * P],
                    rhs=codes[:].bitcast(FP8X4),
                    rhs_scale=plane[:],
                    start=True,
                    stop=True,
                )
            return sums

        def project(t0, t1, grouped, number):
            return multiply(t0, t1, quantise(t0, t1, grouped), number)

        def store_half(t0, t1, h, quantised, number, copy, tag):
            codes, plane = quantised
            sums = bank_tile([P, t1 - t0], number)
            nc.tensor.matmul_mx(
                out=sums[:],
                lhsT=wp_codes[:, h * P : (h + 1) * P].bitcast(FP8X4),
                lhsT_scale=wp_plane[:, h * P : (h + 1) * P],
                rhs=codes[:].bitcast(FP8X4),
                rhs_scale=plane[:],
                start=True,
                stop=True,
            )
            result = keep.tile([P, t1 - t0], F32, name="result", tag=tag, align_bytes=64)
            copy(result[:], sums[:])
            nc.sync.dma_start(out[h * P : (h + 1) * P, t0:t1], result[:])

        def warm_up(number):
            nc.tensor.matmul_mx(
                out=bank_tile([P, 512], number)[:],
                lhsT=wp_codes[:, 0:P].bitcast(FP8X4),
                lhsT_scale=wp_plane[:, 0:P],
                rhs=slot_words[0][:, 0:512].bitcast(FP8X4),
                rhs_scale=slot_bytes[:, 0:512],
                start=True,
                stop=True,
            )

        def store(t0, t1, sums, copy):
            result = keep.tile([P, M // P, t1 - t0], F32, name="result%d" % (t0 // P))
            copy(result[:], sums[:])
            nc.sync.dma_start(out.rearrange("(h p) t -> p h t", p=P)[:, :, t0:t1], result[:])

        def parts_tile(tag, width):
            return keep.tile([P, 2, width], F32, name="parts", tag=tag, align_bytes=64)

        experts(0, (0, 3), (0,))
        experts(1, (0, 3), (4,))
        experts(0, (3, 6, 9), (1, 2))
        experts(0, (9, 10), (3,), on_vector=True)
        experts(1, (3, 7, 10), (5, 6))
        early_parts = [gated(j, P, T, parts_tile("parts%d" % j, T - P)) for j in range(2)]
        fetched = keep.tile([P, 2, NT, P], F32, name="fetched", align_bytes=64)
        experts(2, (0, 3, 5), (7, 0))
        experts(3, (0, 3, 5), (1, 2))
        fetch_first(0, fetched)
        fetch_first(1, fetched)
        experts(2, (5, 8, 10), (3, 4))
        experts(3, (5, 8, 10), (1, 2))
        turned_early = turn_and_add(P, T, early_parts[0], P, 3)
        fetch_first(2, fetched)
        round_turned(0, P, T, turned_early)
        fetch_first(3, fetched)
        first_parts = keep.tile([P, 2, 2, TOKEN_CUTS[1] - TOKEN_CUTS[0]], F32, name="first_parts", align_bytes=64)
        later_parts = keep.tile([P, 2, 2, 2, P], F32, name="later_parts", tag="b_sb", align_bytes=64)
        parts = [first_parts[:], later_parts[:, 0], later_parts[:, 1]]
        for i, (t0, t1) in enumerate(chunks):
            for j in (2, 3):
                gated(j, t0, t1, parts[i][:, j - 2])
        wide, second, third = chunks
        first = (0, P)
        add_turned(1, P, T, early_parts[1], P, 4)
        add_turned(2, *wide, parts[0][:, 0], wide[0], 1)
        scaled, turned = gate_first(fetched, (7, 0))
        add_turned(3, *wide, parts[0][:, 1], wide[0], 2)
        warm_up(4)
        warm_up(7)
        add_first(scaled, turned)
        add_turned(2, *second, parts[1][:, 0], second[0], 5)
        add_turned(3, *second, parts[1][:, 1], second[0], 6)
        grouped_wide = turn_back(*wide, 3)
        add_turned(2, *third, parts[2][:, 0], third[0], 1, nc.vector.tensor_copy)
        add_turned(3, *third, parts[2][:, 1], third[0], 2, nc.vector.tensor_copy)
        grouped_second = turn_back(*second, 4)
        grouped_first = turn_back(*first, 7)
        grouped_third = turn_back(*third, 5)
        order = ((wide, grouped_wide), (second, grouped_second), (first, grouped_first), (third, grouped_third))
        quantised = [quantise(*chunk, grouped) for chunk, grouped in order]
        store_half(*wide, 0, quantised[0], 6, nc.scalar.copy, "result")
        store(*second, multiply(*second, quantised[1], 1), nc.scalar.copy)
        store_half(*wide, 1, quantised[0], 0, nc.vector.tensor_copy, "grouped%d" % (third[0] // P))
        store(*first, multiply(*first, quantised[2], 2), nc.scalar.copy)
        store(*third, multiply(*third, quantised[3], 3), nc.vector.tensor_copy)
